import numpy as np
import ml_dtypes


def mxq(x, axis, fmt="e4m3"):
    dtype, down = {"e4m3": (ml_dtypes.float8_e4m3fn, 7), "e5m2": (ml_dtypes.float8_e5m2, 14)}[fmt]
    v = np.moveaxis(np.asarray(x, np.float32).astype(ml_dtypes.bfloat16).astype(np.float64), axis, -1)
    blocks = v.reshape(v.shape[:-1] + (-1, 32))
    amax = np.abs(blocks).max(-1, keepdims=True)
    byte = np.maximum(np.where(amax > 0, np.frexp(amax)[1] - 1 + 127, 0) - down, 1)
    scale = np.exp2(byte - 127.0)
    codes = (blocks / scale).astype(np.float32).astype(dtype).astype(np.float64)
    return np.moveaxis((codes * scale).reshape(v.shape), -1, axis)


WIDE = False


def mx_kscale(k):
    if not WIDE:
        return np.ones(k)
    levels = np.array([10, -10, 5, -5, 0])
    if k % 512:
        return np.exp2(np.random.permutation(np.resize(levels, k // 32))).repeat(32)
    a = np.empty((k // 512, 16))
    for p in range(k // 512):
        a[p, :8] = np.random.permutation(np.resize(levels, 8))
        for g in range(8):
            far = levels[np.abs(levels - a[p, g]) >= 10]
            a[p, g + 8] = far[np.random.randint(len(far))]
    return np.exp2(a.ravel()).repeat(32)


def f64(x):
    return np.asarray(x).astype(np.float64)


E2M1 = np.array([0.0, 0.5, 1.0, 1.5, 2.0, 3.0, 4.0, 6.0, -0.0, -0.5, -1.0, -1.5, -2.0, -3.0, -4.0, -6.0])


def pack_weight(w, fmt):
    k, n = w.shape
    w = f64(np.asarray(w, np.float32).astype(ml_dtypes.bfloat16)).reshape(k // 32, 32, n)
    amax = np.abs(w).max(1)
    if fmt == "e4m3":
        byte = np.frexp(amax)[1] - 1 + 127 - 7
    else:
        mant, ex = np.frexp(amax / 6.0)
        byte = np.where(mant > 0.5, ex, ex - 1) + 127
    byte = np.clip(np.where(amax > 0, byte, 1), 1, 254)
    scaled = (w * np.exp2(127.0 - byte)[:, None, :]).reshape(k, n).astype(np.float32)
    by_word = np.ascontiguousarray(scaled.reshape(k // 512, 128, 4, n).transpose(0, 1, 3, 2))
    if fmt == "e4m3":
        words = by_word.astype(ml_dtypes.float8_e4m3fn).view(np.uint8)
    else:
        c = by_word.astype(ml_dtypes.float4_e2m1fn).view(np.uint8) & 0xF
        words = (c[..., 0::2] | (c[..., 1::2] << 4)).reshape(k // 512, 128, 2 * n)
    return np.ascontiguousarray(words), np.ascontiguousarray(byte.astype(np.uint8).reshape(k // 512, 16, n))


def unpack_weight(words, scales, fmt):
    g, _, n = scales.shape
    words = np.ascontiguousarray(words).reshape(g, 128, n, -1)
    if fmt == "e4m3":
        vals = words.view(ml_dtypes.float8_e4m3fn).astype(np.float64)
    else:
        nib = np.empty((g, 128, n, 4), np.uint8)
        nib[..., 0::2] = words & 0xF
        nib[..., 1::2] = words >> 4
        vals = E2M1[nib]
    vals = vals * np.repeat(np.exp2(scales.astype(np.float64) - 127.0), 8, axis=1)[..., None]
    return vals.transpose(0, 1, 3, 2).reshape(g * 512, n)


K, M, T = 1024, 1536, 512


def setup_inputs():
    n = np.random.standard_normal
    s = mx_kscale(K)[:, None]
    w = n((K, M)) / np.sqrt(K) / s
    w4 = pack_weight(w, "e2m1")
    rest = w - unpack_weight(*w4, "e2m1")
    p_r8 = pack_weight(rest, "e4m3")
    return {
        "x": (n((K, T)) * s).astype(np.float32),
        "w4_words": w4[0],
        "w4_scales": w4[1],
        "r8_words": p_r8[0],
        "r8_scales": p_r8[1],
    }


def reference(x, w4_words, w4_scales, r8_words, r8_scales):
    x_ = mxq(f64(x), 0, "e4m3")
    w4_ = unpack_weight(w4_words, w4_scales, "e2m1")
    r8_ = unpack_weight(r8_words, r8_scales, "e4m3")
    y = w4_.T @ x_ + r8_.T @ x_
    return np.maximum(y, 0.0) ** 2

@@ -1,0 +1,172 @@
+from contextlib import ExitStack
+
+import concourse.mybir as mybir
+
+K, N_OUT, T = 1024, 1536, 512
+FLOPS = 2 * (2 * K * N_OUT * T)
+
+F32 = mybir.dt.float32
+BF16 = mybir.dt.bfloat16
+I32 = mybir.dt.int32
+U32 = mybir.dt.uint32
+U8 = mybir.dt.uint8
+E4M3 = mybir.dt.float8_e4m3fn_x4
+E2M1 = mybir.dt.float4_e2m1fn_x4
+ACT = mybir.ActivationFunctionType
+ALU = mybir.AluOpType
+
+P = 128
+PACK = 4
+K_PASS = P * PACK
+PASSES = K // K_PASS
+CHUNK = 256
+VEC_COLS = 160
+BANKS = 8
+
+
+def tile_mix_resid_fm_relu2_kernel(tc, x, w4_words, w4_scales, r8_words, r8_scales, out):
+    nc = tc.nc
+    n_tiles = N_OUT // P
+    first = BANKS * P
+
+    with ExitStack() as ctx:
+        keep = ctx.enter_context(tc.tile_pool(name="keep", bufs=1))
+        work = ctx.enter_context(tc.tile_pool(name="work", bufs=n_tiles))
+        psum = ctx.enter_context(tc.psum_pool(name="psum", bufs=1))
+        ctx.enter_context(tc.manual_schedule())
+
+        one = keep.tile([P, 1], F32, name="one")
+        r8_planes = keep.tile([P, N_OUT], U8, name="r8_planes", align_bytes=64)
+        w4_planes = keep.tile([P, PASSES, N_OUT], U8, name="w4_planes", align_bytes=64)
+        nc.gpsimd.memset(one[:], 0.0)
+        nc.vector.memset(r8_planes[:].bitcast(I32), 0)
+        nc.vector.memset(w4_planes[:].rearrange("p a n -> p (a n)").bitcast(I32), 0)
+        for q in range(4):
+            nc.scalar.dma_start(
+                out=r8_planes[32 * q + 4 : 32 * q + 12, :].bitcast(I32),
+                in_=r8_scales[:, 4 * q : 4 * q + 4, :].bitcast(I32),
+            )
+        for q in range(4):
+            nc.gpsimd.dma_start(
+                out=w4_planes[32 * q : 32 * q + 4, :, :].bitcast(I32),
+                in_=w4_scales[:, 4 * q : 4 * q + 4, :].rearrange("a q n -> q a n").bitcast(I32),
+            )
+        nc.scalar.activation(out=one[:], in_=one[:], func=ACT.Relu)
+
+        x_codes = [keep.tile([P, T], U32, name="x_codes%d" % a, align_bytes=64) for a in range(PASSES)]
+        x_scales = [keep.tile([P, T], U8, name="x_scales%d" % a, align_bytes=64) for a in range(PASSES)]
+        x_raw = {}
+
+        def load_x(a, c):
+            raw = keep.tile([P, PACK, CHUNK], F32, name="x_raw%d_%d" % (a, c))
+            nc.sync.dma_start(
+                out=raw[:],
+                in_=x[a * K_PASS : (a + 1) * K_PASS, c : c + CHUNK].rearrange("(p j) w -> p j w", j=PACK),
+            )
+            x_raw[(a, c)] = raw
+
+        def quantize_x(a, c):
+            raw = x_raw[(a, c)]
+            grouped = keep.tile([P, CHUNK, PACK], BF16, name="x_grouped%d_%d" % (a, c), align_bytes=64)
+            nc.vector.tensor_copy(
+                out=grouped[:, 0:VEC_COLS, :], in_=raw[:, :, 0:VEC_COLS].rearrange("p j w -> p w j")
+            )
+            nc.scalar.copy(
+                out=grouped[:, VEC_COLS:CHUNK, :], in_=raw[:, :, VEC_COLS:CHUNK].rearrange("p j w -> p w j")
+            )
+            nc.vector.quantize_mx(
+                out=x_codes[a][:, c : c + CHUNK].bitcast(E4M3),
+                scales=x_scales[a][:, c : c + CHUNK],
+                in_=grouped[:].rearrange("p w j -> p (w j)"),
+            )
+
+        r8_parts = {}
+        w4_parts = {}
+
+        def load_r8(a, n0, n1):
+            words = keep.tile([P, n1 - n0], U32, name="r8_%d_%d" % (a, n0), align_bytes=64)
+            nc.sync.dma_start(
+                out=words[:].bitcast(I32),
+                in_=r8_words[a].rearrange("p n i -> p (n i)")[:, PACK * n0 : PACK * n1].bitcast(I32),
+            )
+            for m in range(n0 // P, n1 // P):
+                r8_parts[(a, m)] = words[:, m * P - n0 : (m + 1) * P - n0].bitcast(E4M3)
+
+        def load_w4(a, n0, n1):
+            words = keep.tile([P, 2 * (n1 - n0)], U8, name="w4_%d_%d" % (a, n0), align_bytes=64)
+            nc.sync.dma_start(out=words[:].bitcast(I32), in_=w4_words[a][:, 2 * n0 : 2 * n1].bitcast(I32))
+            for m in range(n0 // P, n1 // P):
+                w4_parts[(a, m)] = words[:, 2 * (m * P - n0) : 2 * ((m + 1) * P - n0)].bitcast(E2M1)
+
+        load_x(0, 0)
+        load_x(0, CHUNK)
+        load_r8(0, 0, first // 2)
+        load_r8(0, first // 2, first)
+        load_w4(0, 0, first)
+        load_x(1, 0)
+        load_x(1, CHUNK)
+        load_r8(1, 0, first)
+        load_w4(1, 0, first)
+        load_r8(0, first, N_OUT)
+        load_w4(0, first, N_OUT)
+        load_r8(1, first, N_OUT)
+        load_w4(1, first, N_OUT)
+
+        for a in range(PASSES):
+            for c in range(0, T, CHUNK):
+                quantize_x(a, c)
+
+        acc = {}
+
+        def open_bank(m):
+            bank = psum.tile([P, T], F32, name="bank%d" % (m % BANKS))
+            acc[m] = bank
+
+        def add_r8(m, a, start=False):
+            nc.tensor.matmul_mx(
+                out=acc[m][:],
+                lhsT=r8_parts[(a, m)],
+                lhsT_scale=r8_planes[4 + 4 * a :, m * P : (m + 1) * P],
+                rhs=x_codes[a][:].bitcast(E4M3),
+                rhs_scale=x_scales[a][:],
+                start=start,
+                stop=False,
+            )
+
+        def add_w4(m, a, stop=False):
+            nc.tensor.matmul_mx(
+                out=acc[m][:],
+                lhsT=w4_parts[(a, m)],
+                lhsT_scale=w4_planes[:, a, m * P : (m + 1) * P],
+                rhs=x_codes[a][:].bitcast(E4M3),
+                rhs_scale=x_scales[a][:],
+                start=False,
+                stop=stop,
+            )
+
+        def finish(m, pieces):
+            relu = work.tile([P, T], F32, name="relu")
+            result = work.tile([P, T], F32, name="result")
+            width = T // pieces
+            for c in range(0, T, width):
+                cols = slice(c, c + width)
+                nc.scalar.activation(out=relu[:, cols], in_=acc[m][:, cols], func=ACT.Relu)
+                nc.vector.tensor_tensor(out=result[:, cols], in0=relu[:, cols], in1=relu[:, cols], op=ALU.mult)
+                nc.sync.dma_start(out=out[m * P : (m + 1) * P, cols], in_=result[:, cols])
+
+        for m in range(BANKS):
+            open_bank(m)
+            add_r8(m, 0, start=True)
+        for m in range(BANKS):
+            add_w4(m, 0)
+        for m in range(BANKS):
+            add_r8(m, 1)
+            add_w4(m, 1, stop=True)
+            finish(m, 1)
+        for m in range(BANKS, n_tiles):
+            open_bank(m)
+            add_r8(m, 0, start=True)
+            add_w4(m, 0)
+            add_r8(m, 1)
+            add_w4(m, 1, stop=True)
+            finish(m, 2 if m == n_tiles - 1 else 1)

@@ -19,9 +19,10 @@ P = 128
 PACK = 4
 K_PASS = P * PACK
 PASSES = K // K_PASS
-CHUNK = 256
-VEC_COLS = 160
+HALF = T // 2
 BANKS = 8
+EARLY = 5
+LAST_GROUPS = ((0, 256), (256, 128), (384, 128))
 
 
 def tile_mix_resid_fm_relu2_kernel(tc, x, w4_words, w4_scales, r8_words, r8_scales, out):
@@ -31,52 +32,58 @@ def tile_mix_resid_fm_relu2_kernel(tc, x, w4_words, w4_scales, r8_words, r8_scal
 
     with ExitStack() as ctx:
         keep = ctx.enter_context(tc.tile_pool(name="keep", bufs=1))
-        work = ctx.enter_context(tc.tile_pool(name="work", bufs=n_tiles))
+        work = ctx.enter_context(tc.tile_pool(name="work", bufs=n_tiles + 3))
         psum = ctx.enter_context(tc.psum_pool(name="psum", bufs=1))
         ctx.enter_context(tc.manual_schedule())
 
         one = keep.tile([P, 1], F32, name="one")
-        r8_planes = keep.tile([P, N_OUT], U8, name="r8_planes", align_bytes=64)
+        r8_planes = [keep.tile([P, N_OUT], U8, name="r8_planes%d" % a, align_bytes=64) for a in range(PASSES)]
         w4_planes = keep.tile([P, PASSES, N_OUT], U8, name="w4_planes", align_bytes=64)
         nc.gpsimd.memset(one[:], 0.0)
-        nc.vector.memset(r8_planes[:].bitcast(I32), 0)
-        nc.vector.memset(w4_planes[:].rearrange("p a n -> p (a n)").bitcast(I32), 0)
-        for q in range(4):
-            nc.scalar.dma_start(
-                out=r8_planes[32 * q + 4 : 32 * q + 12, :].bitcast(I32),
-                in_=r8_scales[:, 4 * q : 4 * q + 4, :].bitcast(I32),
-            )
-        for q in range(4):
-            nc.gpsimd.dma_start(
-                out=w4_planes[32 * q : 32 * q + 4, :, :].bitcast(I32),
-                in_=w4_scales[:, 4 * q : 4 * q + 4, :].rearrange("a q n -> q a n").bitcast(I32),
-            )
         nc.scalar.activation(out=one[:], in_=one[:], func=ACT.Relu)
+        nc.vector.memset(w4_planes[:].rearrange("p a n -> p (a n)").bitcast(I32), 0)
+        for a in range(PASSES):
+            nc.vector.memset(r8_planes[a][:].bitcast(I32), 0)
+        for r in range(4):
+            nc.gpsimd.dma_start(
+                out=w4_planes[r:P:32, :, :].bitcast(I32),
+                in_=w4_scales.rearrange("a (q r) n -> r q a n", r=4)[r].bitcast(I32),
+            )
+
+        def load_r8_scales(a):
+            for r in range(4):
+                nc.sync.dma_start(
+                    out=r8_planes[a][4 + 4 * a + r : P : 32, :].bitcast(I32),
+                    in_=r8_scales[a].rearrange("(q r) n -> r q n", r=4)[r].bitcast(I32),
+                )
 
         x_codes = [keep.tile([P, T], U32, name="x_codes%d" % a, align_bytes=64) for a in range(PASSES)]
         x_scales = [keep.tile([P, T], U8, name="x_scales%d" % a, align_bytes=64) for a in range(PASSES)]
         x_raw = {}
 
-        def load_x(a, c):
-            raw = keep.tile([P, PACK, CHUNK], F32, name="x_raw%d_%d" % (a, c))
+        def load_x(a, c0, c1):
+            raw = keep.tile([P, PACK, c1 - c0], F32, name="x_raw%d_%d" % (a, c0))
             nc.sync.dma_start(
                 out=raw[:],
-                in_=x[a * K_PASS : (a + 1) * K_PASS, c : c + CHUNK].rearrange("(p j) w -> p j w", j=PACK),
+                in_=x[a * K_PASS : (a + 1) * K_PASS, c0:c1].rearrange("(p j) w -> p j w", j=PACK),
             )
-            x_raw[(a, c)] = raw
+            for c in range(c0, c1, HALF):
+                x_raw[(a, c)] = raw[:, :, c - c0 : c - c0 + HALF]
 
-        def quantize_x(a, c):
+        def quantize_x(a, c, vec_cols):
             raw = x_raw[(a, c)]
-            grouped = keep.tile([P, CHUNK, PACK], BF16, name="x_grouped%d_%d" % (a, c), align_bytes=64)
+            grouped = keep.tile([P, HALF, PACK], BF16, name="x_grouped%d_%d" % (a, c), align_bytes=64)
             nc.vector.tensor_copy(
-                out=grouped[:, 0:VEC_COLS, :], in_=raw[:, :, 0:VEC_COLS].rearrange("p j w -> p w j")
+                out=grouped[:, 0:vec_cols, :].rearrange("p (c i) j -> p c j i", i=4),
+                in_=raw[:, :, 0:vec_cols].rearrange("p j (c i) -> p c j i", i=4),
             )
             nc.scalar.copy(
-                out=grouped[:, VEC_COLS:CHUNK, :], in_=raw[:, :, VEC_COLS:CHUNK].rearrange("p j w -> p w j")
+                out=grouped[:, vec_cols:HALF, :].rearrange("p (c i) j -> p c j i", i=4),
+                in_=raw[:, :, vec_cols:HALF].rearrange("p j (c i) -> p c j i", i=4),
             )
             nc.vector.quantize_mx(
-                out=x_codes[a][:, c : c + CHUNK].bitcast(E4M3),
-                scales=x_scales[a][:, c : c + CHUNK],
+                out=x_codes[a][:, c : c + HALF].bitcast(E4M3),
+                scales=x_scales[a][:, c : c + HALF],
                 in_=grouped[:].rearrange("p w j -> p (w j)"),
             )
 
@@ -98,75 +105,92 @@ def tile_mix_resid_fm_relu2_kernel(tc, x, w4_words, w4_scales, r8_words, r8_scal
             for m in range(n0 // P, n1 // P):
                 w4_parts[(a, m)] = words[:, 2 * (m * P - n0) : 2 * ((m + 1) * P - n0)].bitcast(E2M1)
 
-        load_x(0, 0)
-        load_x(0, CHUNK)
+        load_x(0, 0, HALF)
+        load_r8_scales(0)
         load_r8(0, 0, first // 2)
+        load_x(0, HALF, T)
         load_r8(0, first // 2, first)
         load_w4(0, 0, first)
-        load_x(1, 0)
-        load_x(1, CHUNK)
-        load_r8(1, 0, first)
+        load_x(1, 0, T)
+        load_r8_scales(1)
+        load_r8(1, 0, first // 2)
+        load_r8(1, first // 2, first)
         load_w4(1, 0, first)
         load_r8(0, first, N_OUT)
         load_w4(0, first, N_OUT)
         load_r8(1, first, N_OUT)
         load_w4(1, first, N_OUT)
 
-        for a in range(PASSES):
-            for c in range(0, T, CHUNK):
-                quantize_x(a, c)
+        quantize_x(0, 0, 168)
+        quantize_x(0, HALF, 168)
+        quantize_x(1, 0, 168)
+        quantize_x(1, HALF, 120)
 
-        acc = {}
+        def open_bank(b):
+            bank = psum.tile([P, T], F32, name="bank%d" % b)
+            return bank
 
-        def open_bank(m):
-            bank = psum.tile([P, T], F32, name="bank%d" % (m % BANKS))
-            acc[m] = bank
-
-        def add_r8(m, a, start=False):
+        def add_r8(acc, m, a, c, width, start=False):
             nc.tensor.matmul_mx(
-                out=acc[m][:],
+                out=acc,
                 lhsT=r8_parts[(a, m)],
-                lhsT_scale=r8_planes[4 + 4 * a :, m * P : (m + 1) * P],
-                rhs=x_codes[a][:].bitcast(E4M3),
-                rhs_scale=x_scales[a][:],
+                lhsT_scale=r8_planes[a][4 + 4 * a :, m * P : (m + 1) * P],
+                rhs=x_codes[a][:, c : c + width].bitcast(E4M3),
+                rhs_scale=x_scales[a][:, c : c + width],
                 start=start,
                 stop=False,
             )
 
-        def add_w4(m, a, stop=False):
+        def add_w4(acc, m, a, c, width, stop=False):
             nc.tensor.matmul_mx(
-                out=acc[m][:],
+                out=acc,
                 lhsT=w4_parts[(a, m)],
                 lhsT_scale=w4_planes[:, a, m * P : (m + 1) * P],
-                rhs=x_codes[a][:].bitcast(E4M3),
-                rhs_scale=x_scales[a][:],
+                rhs=x_codes[a][:, c : c + width].bitcast(E4M3),
+                rhs_scale=x_scales[a][:, c : c + width],
                 start=False,
                 stop=stop,
             )
 
-        def finish(m, pieces):
+        def finish(acc, m, c, width):
             relu = work.tile([P, T], F32, name="relu")
             result = work.tile([P, T], F32, name="result")
-            width = T // pieces
-            for c in range(0, T, width):
-                cols = slice(c, c + width)
-                nc.scalar.activation(out=relu[:, cols], in_=acc[m][:, cols], func=ACT.Relu)
-                nc.vector.tensor_tensor(out=result[:, cols], in0=relu[:, cols], in1=relu[:, cols], op=ALU.mult)
-                nc.sync.dma_start(out=out[m * P : (m + 1) * P, cols], in_=result[:, cols])
+            nc.scalar.activation(out=relu[:, 0:width], in_=acc, func=ACT.Relu)
+            nc.vector.tensor_tensor(out=result[:, 0:width], in0=relu[:, 0:width], in1=relu[:, 0:width], op=ALU.mult)
+            nc.sync.dma_start(out=out[m * P : (m + 1) * P, c : c + width], in_=result[:, 0:width])
 
+        banks = [open_bank(m) for m in range(BANKS)]
         for m in range(BANKS):
-            open_bank(m)
-            add_r8(m, 0, start=True)
+            add_r8(banks[m][:, 0:HALF], m, 0, 0, HALF, start=True)
         for m in range(BANKS):
-            add_w4(m, 0)
+            add_r8(banks[m][:, HALF:T], m, 0, HALF, HALF)
         for m in range(BANKS):
-            add_r8(m, 1)
-            add_w4(m, 1, stop=True)
-            finish(m, 1)
-        for m in range(BANKS, n_tiles):
-            open_bank(m)
-            add_r8(m, 0, start=True)
-            add_w4(m, 0)
-            add_r8(m, 1)
-            add_w4(m, 1, stop=True)
-            finish(m, 2 if m == n_tiles - 1 else 1)
+            add_w4(banks[m][:], m, 0, 0, T)
+        for m in range(EARLY):
+            add_r8(banks[m][:, 0:HALF], m, 1, 0, HALF)
+        for m in range(BANKS):
+            if m < EARLY:
+                add_r8(banks[m][:, HALF:T], m, 1, HALF, HALF)
+            else:
+                add_r8(banks[m][:], m, 1, 0, T)
+            add_w4(banks[m][:], m, 1, 0, T, stop=True)
+            finish(banks[m][:], m, 0, T)
+        for m in range(BANKS, n_tiles - 1):
+            bank = open_bank(m - BANKS)
+            add_r8(bank[:], m, 0, 0, T, start=True)
+            add_w4(bank[:], m, 0, 0, T)
+            add_r8(bank[:], m, 1, 0, T)
+            add_w4(bank[:], m, 1, 0, T, stop=True)
+            if m < n_tiles - 2:
+                finish(bank[:], m, 0, T)
+            else:
+                finish(bank[:, 0:HALF], m, 0, HALF)
+                finish(bank[:, HALF:T], m, HALF, HALF)
+        m = n_tiles - 1
+        for g, (c, width) in enumerate(LAST_GROUPS):
+            bank = open_bank(m - BANKS + g)
+            for a in range(PASSES):
+                add_r8(bank[:, 0:width], m, a, c, width, start=(a == 0))
+                for d in range(0, width, P):
+                    add_w4(bank[:, d : d + P], m, a, c + d, P, stop=(a == PASSES - 1 and d == width - P))
+            finish(bank[:, 0:width], m, c, width)

@@ -21,7 +21,7 @@ K_PASS = P * PACK
 PASSES = K // K_PASS
 HALF = T // 2
 BANKS = 8
-EARLY = 5
+EARLY = 4
 LAST_GROUPS = ((0, 256), (256, 128), (384, 128))
 
 
@@ -38,24 +38,22 @@ def tile_mix_resid_fm_relu2_kernel(tc, x, w4_words, w4_scales, r8_words, r8_scal
 
         one = keep.tile([P, 1], F32, name="one")
         r8_planes = [keep.tile([P, N_OUT], U8, name="r8_planes%d" % a, align_bytes=64) for a in range(PASSES)]
-        w4_planes = keep.tile([P, PASSES, N_OUT], U8, name="w4_planes", align_bytes=64)
+        w4_planes = [keep.tile([P, N_OUT], U8, name="w4_planes%d" % a, align_bytes=64) for a in range(PASSES)]
         nc.gpsimd.memset(one[:], 0.0)
         nc.scalar.activation(out=one[:], in_=one[:], func=ACT.Relu)
-        nc.vector.memset(w4_planes[:].rearrange("p a n -> p (a n)").bitcast(I32), 0)
-        for a in range(PASSES):
-            nc.vector.memset(r8_planes[a][:].bitcast(I32), 0)
-        for r in range(4):
-            nc.gpsimd.dma_start(
-                out=w4_planes[r:P:32, :, :].bitcast(I32),
-                in_=w4_scales.rearrange("a (q r) n -> r q a n", r=4)[r].bitcast(I32),
-            )
+        nc.gpsimd.memset(w4_planes[0][:].bitcast(I32), 0)
+        for plane in r8_planes + w4_planes[1:]:
+            nc.vector.memset(plane[:].bitcast(I32), 0)
 
-        def load_r8_scales(a):
+        def load_scales(queue, plane, row0, scales):
             for r in range(4):
-                nc.sync.dma_start(
-                    out=r8_planes[a][4 + 4 * a + r : P : 32, :].bitcast(I32),
-                    in_=r8_scales[a].rearrange("(q r) n -> r q n", r=4)[r].bitcast(I32),
+                queue.dma_start(
+                    out=plane[row0 + r : P : 32, :].bitcast(I32),
+                    in_=scales.rearrange("(q r) n -> r q n", r=4)[r].bitcast(I32),
                 )
+
+        load_scales(nc.gpsimd, w4_planes[0], 0, w4_scales[0])
+        load_scales(nc.gpsimd, r8_planes[1], 8, r8_scales[1])
 
         x_codes = [keep.tile([P, T], U32, name="x_codes%d" % a, align_bytes=64) for a in range(PASSES)]
         x_scales = [keep.tile([P, T], U8, name="x_scales%d" % a, align_bytes=64) for a in range(PASSES)]
@@ -106,25 +104,23 @@ def tile_mix_resid_fm_relu2_kernel(tc, x, w4_words, w4_scales, r8_words, r8_scal
                 w4_parts[(a, m)] = words[:, 2 * (m * P - n0) : 2 * ((m + 1) * P - n0)].bitcast(E2M1)
 
         load_x(0, 0, HALF)
-        load_r8_scales(0)
+        load_scales(nc.sync, r8_planes[0], 4, r8_scales[0])
         load_r8(0, 0, first // 2)
         load_x(0, HALF, T)
         load_r8(0, first // 2, first)
         load_w4(0, 0, first)
-        load_x(1, 0, T)
-        load_r8_scales(1)
+        load_x(1, 0, HALF)
+        load_x(1, HALF, T)
         load_r8(1, 0, first // 2)
-        load_r8(1, first // 2, first)
-        load_w4(1, 0, first)
+        load_scales(nc.sync, w4_planes[1], 0, w4_scales[1])
+        load_w4(1, 0, N_OUT)
+        load_r8(1, first // 2, N_OUT)
         load_r8(0, first, N_OUT)
         load_w4(0, first, N_OUT)
-        load_r8(1, first, N_OUT)
-        load_w4(1, first, N_OUT)
 
-        quantize_x(0, 0, 168)
-        quantize_x(0, HALF, 168)
-        quantize_x(1, 0, 168)
-        quantize_x(1, HALF, 120)
+        for a in range(PASSES):
+            for c in range(0, T, HALF):
+                quantize_x(a, c, 168)
 
         def open_bank(b):
             bank = psum.tile([P, T], F32, name="bank%d" % b)
@@ -145,7 +141,7 @@ def tile_mix_resid_fm_relu2_kernel(tc, x, w4_words, w4_scales, r8_words, r8_scal
             nc.tensor.matmul_mx(
                 out=acc,
                 lhsT=w4_parts[(a, m)],
-                lhsT_scale=w4_planes[:, a, m * P : (m + 1) * P],
+                lhsT_scale=w4_planes[a][:, m * P : (m + 1) * P],
                 rhs=x_codes[a][:, c : c + width].bitcast(E4M3),
                 rhs_scale=x_scales[a][:, c : c + width],
                 start=False,

@@ -113,8 +113,9 @@ def tile_mix_resid_fm_relu2_kernel(tc, x, w4_words, w4_scales, r8_words, r8_scal
         load_x(1, HALF, T)
         load_r8(1, 0, first // 2)
         load_scales(nc.sync, w4_planes[1], 0, w4_scales[1])
-        load_w4(1, 0, N_OUT)
+        load_w4(1, 0, first // 2)
         load_r8(1, first // 2, N_OUT)
+        load_w4(1, first // 2, N_OUT)
         load_r8(0, first, N_OUT)
         load_w4(0, first, N_OUT)
 
@@ -164,10 +165,10 @@ def tile_mix_resid_fm_relu2_kernel(tc, x, w4_words, w4_scales, r8_words, r8_scal
             add_w4(banks[m][:], m, 0, 0, T)
         for m in range(EARLY):
             add_r8(banks[m][:, 0:HALF], m, 1, 0, HALF)
+        for m in range(EARLY):
+            add_r8(banks[m][:, HALF:T], m, 1, HALF, HALF)
         for m in range(BANKS):
-            if m < EARLY:
-                add_r8(banks[m][:, HALF:T], m, 1, HALF, HALF)
-            else:
+            if m >= EARLY:
                 add_r8(banks[m][:], m, 1, 0, T)
             add_w4(banks[m][:], m, 1, 0, T, stop=True)
             finish(banks[m][:], m, 0, T)

@@ -41,8 +41,7 @@ def tile_mix_resid_fm_relu2_kernel(tc, x, w4_words, w4_scales, r8_words, r8_scal
         w4_planes = [keep.tile([P, N_OUT], U8, name="w4_planes%d" % a, align_bytes=64) for a in range(PASSES)]
         nc.gpsimd.memset(one[:], 0.0)
         nc.scalar.activation(out=one[:], in_=one[:], func=ACT.Relu)
-        nc.gpsimd.memset(w4_planes[0][:].bitcast(I32), 0)
-        for plane in r8_planes + w4_planes[1:]:
+        for plane in r8_planes + w4_planes:
             nc.vector.memset(plane[:].bitcast(I32), 0)
 
         def load_scales(queue, plane, row0, scales):
@@ -52,7 +51,6 @@ def tile_mix_resid_fm_relu2_kernel(tc, x, w4_words, w4_scales, r8_words, r8_scal
                     in_=scales.rearrange("(q r) n -> r q n", r=4)[r].bitcast(I32),
                 )
 
-        load_scales(nc.gpsimd, w4_planes[0], 0, w4_scales[0])
         load_scales(nc.gpsimd, r8_planes[1], 8, r8_scales[1])
 
         x_codes = [keep.tile([P, T], U32, name="x_codes%d" % a, align_bytes=64) for a in range(PASSES)]
@@ -108,6 +106,7 @@ def tile_mix_resid_fm_relu2_kernel(tc, x, w4_words, w4_scales, r8_words, r8_scal
         load_r8(0, 0, first // 2)
         load_x(0, HALF, T)
         load_r8(0, first // 2, first)
+        load_scales(nc.sync, w4_planes[0], 0, w4_scales[0])
         load_w4(0, 0, first)
         load_x(1, 0, HALF)
         load_x(1, HALF, T)

@@ -21,6 +21,7 @@ K_PASS = P * PACK
 PASSES = K // K_PASS
 HALF = T // 2
 BANKS = 8
+ALIGN = 256
 EARLY = 4
 LAST_GROUPS = ((0, 256), (256, 128), (384, 128))
 
@@ -37,8 +38,8 @@ def tile_mix_resid_fm_relu2_kernel(tc, x, w4_words, w4_scales, r8_words, r8_scal
         ctx.enter_context(tc.manual_schedule())
 
         one = keep.tile([P, 1], F32, name="one")
-        r8_planes = [keep.tile([P, N_OUT], U8, name="r8_planes%d" % a, align_bytes=64) for a in range(PASSES)]
-        w4_planes = [keep.tile([P, N_OUT], U8, name="w4_planes%d" % a, align_bytes=64) for a in range(PASSES)]
+        r8_planes = [keep.tile([P, N_OUT], U8, name="r8_planes%d" % a, align_bytes=ALIGN) for a in range(PASSES)]
+        w4_planes = [keep.tile([P, N_OUT], U8, name="w4_planes%d" % a, align_bytes=ALIGN) for a in range(PASSES)]
         nc.gpsimd.memset(one[:], 0.0)
         nc.scalar.activation(out=one[:], in_=one[:], func=ACT.Relu)
         for plane in r8_planes + w4_planes:
@@ -53,12 +54,12 @@ def tile_mix_resid_fm_relu2_kernel(tc, x, w4_words, w4_scales, r8_words, r8_scal
 
         load_scales(nc.gpsimd, r8_planes[1], 8, r8_scales[1])
 
-        x_codes = [keep.tile([P, T], U32, name="x_codes%d" % a, align_bytes=64) for a in range(PASSES)]
-        x_scales = [keep.tile([P, T], U8, name="x_scales%d" % a, align_bytes=64) for a in range(PASSES)]
+        x_codes = [keep.tile([P, T], U32, name="x_codes%d" % a, align_bytes=ALIGN) for a in range(PASSES)]
+        x_scales = [keep.tile([P, T], U8, name="x_scales%d" % a, align_bytes=ALIGN) for a in range(PASSES)]
         x_raw = {}
 
         def load_x(a, c0, c1):
-            raw = keep.tile([P, PACK, c1 - c0], F32, name="x_raw%d_%d" % (a, c0))
+            raw = keep.tile([P, PACK, c1 - c0], F32, name="x_raw%d_%d" % (a, c0), align_bytes=ALIGN)
             nc.sync.dma_start(
                 out=raw[:],
                 in_=x[a * K_PASS : (a + 1) * K_PASS, c0:c1].rearrange("(p j) w -> p j w", j=PACK),
@@ -68,7 +69,7 @@ def tile_mix_resid_fm_relu2_kernel(tc, x, w4_words, w4_scales, r8_words, r8_scal
 
         def quantize_x(a, c, vec_cols):
             raw = x_raw[(a, c)]
-            grouped = keep.tile([P, HALF, PACK], BF16, name="x_grouped%d_%d" % (a, c), align_bytes=64)
+            grouped = keep.tile([P, HALF, PACK], BF16, name="x_grouped%d_%d" % (a, c), align_bytes=ALIGN)
             nc.vector.tensor_copy(
                 out=grouped[:, 0:vec_cols, :].rearrange("p (c i) j -> p c j i", i=4),
                 in_=raw[:, :, 0:vec_cols].rearrange("p j (c i) -> p c j i", i=4),
@@ -87,7 +88,7 @@ def tile_mix_resid_fm_relu2_kernel(tc, x, w4_words, w4_scales, r8_words, r8_scal
         w4_parts = {}
 
         def load_r8(a, n0, n1):
-            words = keep.tile([P, n1 - n0], U32, name="r8_%d_%d" % (a, n0), align_bytes=64)
+            words = keep.tile([P, n1 - n0], U32, name="r8_%d_%d" % (a, n0), align_bytes=ALIGN)
             nc.sync.dma_start(
                 out=words[:].bitcast(I32),
                 in_=r8_words[a].rearrange("p n i -> p (n i)")[:, PACK * n0 : PACK * n1].bitcast(I32),
@@ -96,7 +97,7 @@ def tile_mix_resid_fm_relu2_kernel(tc, x, w4_words, w4_scales, r8_words, r8_scal
                 r8_parts[(a, m)] = words[:, m * P - n0 : (m + 1) * P - n0].bitcast(E4M3)
 
         def load_w4(a, n0, n1):
-            words = keep.tile([P, 2 * (n1 - n0)], U8, name="w4_%d_%d" % (a, n0), align_bytes=64)
+            words = keep.tile([P, 2 * (n1 - n0)], U8, name="w4_%d_%d" % (a, n0), align_bytes=ALIGN)
             nc.sync.dma_start(out=words[:].bitcast(I32), in_=w4_words[a][:, 2 * n0 : 2 * n1].bitcast(I32))
             for m in range(n0 // P, n1 // P):
                 w4_parts[(a, m)] = words[:, 2 * (m * P - n0) : 2 * ((m + 1) * P - n0)].bitcast(E2M1)
@@ -149,8 +150,8 @@ def tile_mix_resid_fm_relu2_kernel(tc, x, w4_words, w4_scales, r8_words, r8_scal
             )
 
         def finish(acc, m, c, width):
-            relu = work.tile([P, T], F32, name="relu")
-            result = work.tile([P, T], F32, name="result")
+            relu = work.tile([P, T], F32, name="relu", align_bytes=ALIGN)
+            result = work.tile([P, T], F32, name="result", align_bytes=ALIGN)
             nc.scalar.activation(out=relu[:, 0:width], in_=acc, func=ACT.Relu)
             nc.vector.tensor_tensor(out=result[:, 0:width], in0=relu[:, 0:width], in1=relu[:, 0:width], op=ALU.mult)
             nc.sync.dma_start(out=out[m * P : (m + 1) * P, c : c + width], in_=result[:, 0:width])

@@ -22,6 +22,8 @@ PASSES = K // K_PASS
 HALF = T // 2
 BANKS = 8
 ALIGN = 256
+PLANES = 4
+PLANE_COLS = N_OUT // PLANES
 EARLY = 4
 LAST_GROUPS = ((0, 256), (256, 128), (384, 128))
 
@@ -38,11 +40,11 @@ def tile_mix_resid_fm_relu2_kernel(tc, x, w4_words, w4_scales, r8_words, r8_scal
         ctx.enter_context(tc.manual_schedule())
 
         one = keep.tile([P, 1], F32, name="one")
-        r8_planes = [keep.tile([P, N_OUT], U8, name="r8_planes%d" % a, align_bytes=ALIGN) for a in range(PASSES)]
+        r8_planes = [keep.tile([P, PLANE_COLS], U8, name="r8_planes%d" % a, align_bytes=ALIGN) for a in range(PASSES)]
         w4_planes = [keep.tile([P, N_OUT], U8, name="w4_planes%d" % a, align_bytes=ALIGN) for a in range(PASSES)]
         nc.gpsimd.memset(one[:], 0.0)
         nc.scalar.activation(out=one[:], in_=one[:], func=ACT.Relu)
-        for plane in r8_planes + w4_planes:
+        for plane in (r8_planes[1], w4_planes[0], r8_planes[0], w4_planes[1]):
             nc.vector.memset(plane[:].bitcast(I32), 0)
 
         def load_scales(queue, plane, row0, scales):
@@ -52,7 +54,14 @@ def tile_mix_resid_fm_relu2_kernel(tc, x, w4_words, w4_scales, r8_words, r8_scal
                     in_=scales.rearrange("(q r) n -> r q n", r=4)[r].bitcast(I32),
                 )
 
-        load_scales(nc.gpsimd, r8_planes[1], 8, r8_scales[1])
+        def load_packed_scales(queue, planes, scales):
+            for q in range(4):
+                queue.dma_start(
+                    out=planes[32 * q : 32 * q + 4 * PLANES, :].bitcast(I32),
+                    in_=scales[4 * q : 4 * q + 4, :].rearrange("r (c n) -> c r n", c=PLANES).bitcast(I32),
+                )
+
+        load_packed_scales(nc.gpsimd, r8_planes[1], r8_scales[1])
 
         x_codes = [keep.tile([P, T], U32, name="x_codes%d" % a, align_bytes=ALIGN) for a in range(PASSES)]
         x_scales = [keep.tile([P, T], U8, name="x_scales%d" % a, align_bytes=ALIGN) for a in range(PASSES)]
@@ -70,19 +79,22 @@ def tile_mix_resid_fm_relu2_kernel(tc, x, w4_words, w4_scales, r8_words, r8_scal
         def quantize_x(a, c, vec_cols):
             raw = x_raw[(a, c)]
             grouped = keep.tile([P, HALF, PACK], BF16, name="x_grouped%d_%d" % (a, c), align_bytes=ALIGN)
-            nc.vector.tensor_copy(
-                out=grouped[:, 0:vec_cols, :].rearrange("p (c i) j -> p c j i", i=4),
-                in_=raw[:, :, 0:vec_cols].rearrange("p j (c i) -> p c j i", i=4),
-            )
-            nc.scalar.copy(
-                out=grouped[:, vec_cols:HALF, :].rearrange("p (c i) j -> p c j i", i=4),
-                in_=raw[:, :, vec_cols:HALF].rearrange("p j (c i) -> p c j i", i=4),
-            )
-            nc.vector.quantize_mx(
-                out=x_codes[a][:, c : c + HALF].bitcast(E4M3),
-                scales=x_scales[a][:, c : c + HALF],
-                in_=grouped[:].rearrange("p w j -> p (w j)"),
-            )
+
+            def interleave(copy, c0, c1):
+                copy(
+                    out=grouped[:, c0:c1, :].rearrange("p (c i) j -> p c j i", i=4),
+                    in_=raw[:, :, c0:c1].rearrange("p j (c i) -> p c j i", i=4),
+                )
+
+            interleave(nc.vector.tensor_copy, 0, P)
+            interleave(nc.vector.tensor_copy, P, vec_cols)
+            interleave(nc.scalar.copy, vec_cols, HALF)
+            for d in range(0, HALF, P):
+                nc.vector.quantize_mx(
+                    out=x_codes[a][:, c + d : c + d + P].bitcast(E4M3),
+                    scales=x_scales[a][:, c + d : c + d + P],
+                    in_=grouped[:, d : d + P, :].rearrange("p w j -> p (w j)"),
+                )
 
         r8_parts = {}
         w4_parts = {}
@@ -103,12 +115,11 @@ def tile_mix_resid_fm_relu2_kernel(tc, x, w4_words, w4_scales, r8_words, r8_scal
                 w4_parts[(a, m)] = words[:, 2 * (m * P - n0) : 2 * ((m + 1) * P - n0)].bitcast(E2M1)
 
         load_x(0, 0, HALF)
-        load_scales(nc.sync, r8_planes[0], 4, r8_scales[0])
-        load_r8(0, 0, first // 2)
-        load_x(0, HALF, T)
-        load_r8(0, first // 2, first)
         load_scales(nc.sync, w4_planes[0], 0, w4_scales[0])
         load_w4(0, 0, first)
+        load_x(0, HALF, T)
+        load_packed_scales(nc.sync, r8_planes[0], r8_scales[0])
+        load_r8(0, 0, first)
         load_x(1, 0, HALF)
         load_x(1, HALF, T)
         load_r8(1, 0, first // 2)
@@ -131,21 +142,21 @@ def tile_mix_resid_fm_relu2_kernel(tc, x, w4_words, w4_scales, r8_words, r8_scal
             nc.tensor.matmul_mx(
                 out=acc,
                 lhsT=r8_parts[(a, m)],
-                lhsT_scale=r8_planes[a][4 + 4 * a :, m * P : (m + 1) * P],
+                lhsT_scale=r8_planes[a][4 * (m * P // PLANE_COLS) :, m * P % PLANE_COLS : m * P % PLANE_COLS + P],
                 rhs=x_codes[a][:, c : c + width].bitcast(E4M3),
                 rhs_scale=x_scales[a][:, c : c + width],
                 start=start,
                 stop=False,
             )
 
-        def add_w4(acc, m, a, c, width, stop=False):
+        def add_w4(acc, m, a, c, width, start=False, stop=False):
             nc.tensor.matmul_mx(
                 out=acc,
                 lhsT=w4_parts[(a, m)],
                 lhsT_scale=w4_planes[a][:, m * P : (m + 1) * P],
                 rhs=x_codes[a][:, c : c + width].bitcast(E4M3),
                 rhs_scale=x_scales[a][:, c : c + width],
-                start=False,
+                start=start,
                 stop=stop,
             )
 
@@ -157,12 +168,11 @@ def tile_mix_resid_fm_relu2_kernel(tc, x, w4_words, w4_scales, r8_words, r8_scal
             nc.sync.dma_start(out=out[m * P : (m + 1) * P, c : c + width], in_=result[:, 0:width])
 
         banks = [open_bank(m) for m in range(BANKS)]
+        for c in range(0, T, P):
+            for m in range(BANKS):
+                add_w4(banks[m][:, c : c + P], m, 0, c, P, start=(c == 0))
         for m in range(BANKS):
-            add_r8(banks[m][:, 0:HALF], m, 0, 0, HALF, start=True)
-        for m in range(BANKS):
-            add_r8(banks[m][:, HALF:T], m, 0, HALF, HALF)
-        for m in range(BANKS):
-            add_w4(banks[m][:], m, 0, 0, T)
+            add_r8(banks[m][:], m, 0, 0, T)
         for m in range(EARLY):
             add_r8(banks[m][:, 0:HALF], m, 1, 0, HALF)
         for m in range(EARLY):

@@ -114,6 +114,22 @@ def tile_mix_resid_fm_relu2_kernel(tc, x, w4_words, w4_scales, r8_words, r8_scal
             for m in range(n0 // P, n1 // P):
                 w4_parts[(a, m)] = words[:, 2 * (m * P - n0) : 2 * ((m + 1) * P - n0)].bitcast(E2M1)
 
+        def load_rest():
+            r8_rest = keep.tile([P, PASSES, N_OUT - first], U32, name="r8_rest", align_bytes=ALIGN)
+            nc.sync.dma_start(
+                out=r8_rest[:].bitcast(I32),
+                in_=r8_words.rearrange("a p n i -> p a (n i)")[:, :, PACK * first :].bitcast(I32),
+            )
+            w4_rest = keep.tile([P, PASSES, 2 * (N_OUT - first)], U8, name="w4_rest", align_bytes=ALIGN)
+            nc.sync.dma_start(
+                out=w4_rest[:].bitcast(I32),
+                in_=w4_words.rearrange("a p n -> p a n")[:, :, 2 * first :].bitcast(I32),
+            )
+            for a in range(PASSES):
+                for m in range(BANKS, n_tiles):
+                    r8_parts[(a, m)] = r8_rest[:, a, m * P - first : (m + 1) * P - first].bitcast(E4M3)
+                    w4_parts[(a, m)] = w4_rest[:, a, 2 * (m * P - first) : 2 * ((m + 1) * P - first)].bitcast(E2M1)
+
         load_x(0, 0, HALF)
         load_scales(nc.sync, w4_planes[0], 0, w4_scales[0])
         load_w4(0, 0, first)
@@ -124,11 +140,9 @@ def tile_mix_resid_fm_relu2_kernel(tc, x, w4_words, w4_scales, r8_words, r8_scal
         load_x(1, HALF, T)
         load_r8(1, 0, first // 2)
         load_scales(nc.sync, w4_planes[1], 0, w4_scales[1])
-        load_w4(1, 0, first // 2)
-        load_r8(1, first // 2, N_OUT)
-        load_w4(1, first // 2, N_OUT)
-        load_r8(0, first, N_OUT)
-        load_w4(0, first, N_OUT)
+        load_w4(1, 0, first)
+        load_r8(1, first // 2, first)
+        load_rest()
 
         for a in range(PASSES):
             for c in range(0, T, HALF):
@@ -160,11 +174,13 @@ def tile_mix_resid_fm_relu2_kernel(tc, x, w4_words, w4_scales, r8_words, r8_scal
                 stop=stop,
             )
 
-        def finish(acc, m, c, width):
+        def finish(acc, m, c, width, steps=1):
             relu = work.tile([P, T], F32, name="relu", align_bytes=ALIGN)
             result = work.tile([P, T], F32, name="result", align_bytes=ALIGN)
-            nc.scalar.activation(out=relu[:, 0:width], in_=acc, func=ACT.Relu)
-            nc.vector.tensor_tensor(out=result[:, 0:width], in0=relu[:, 0:width], in1=relu[:, 0:width], op=ALU.mult)
+            for d in range(0, width, width // steps):
+                cols = slice(d, d + width // steps)
+                nc.scalar.activation(out=relu[:, cols], in_=acc[:, cols], func=ACT.Relu)
+                nc.vector.tensor_tensor(out=result[:, cols], in0=relu[:, cols], in1=relu[:, cols], op=ALU.mult)
             nc.sync.dma_start(out=out[m * P : (m + 1) * P, c : c + width], in_=result[:, 0:width])
 
         banks = [open_bank(m) for m in range(BANKS)]
@@ -181,7 +197,7 @@ def tile_mix_resid_fm_relu2_kernel(tc, x, w4_words, w4_scales, r8_words, r8_scal
             if m >= EARLY:
                 add_r8(banks[m][:], m, 1, 0, T)
             add_w4(banks[m][:], m, 1, 0, T, stop=True)
-            finish(banks[m][:], m, 0, T)
+            finish(banks[m][:], m, 0, T, steps=2 if m == 0 else 1)
         for m in range(BANKS, n_tiles - 1):
             bank = open_bank(m - BANKS)
             add_r8(bank[:], m, 0, 0, T, start=True)
@@ -194,10 +210,16 @@ def tile_mix_resid_fm_relu2_kernel(tc, x, w4_words, w4_scales, r8_words, r8_scal
                 finish(bank[:, 0:HALF], m, 0, HALF)
                 finish(bank[:, HALF:T], m, HALF, HALF)
         m = n_tiles - 1
+        last = keep.tile([P, T], F32, name="last", align_bytes=ALIGN)
         for g, (c, width) in enumerate(LAST_GROUPS):
             bank = open_bank(m - BANKS + g)
             for a in range(PASSES):
                 add_r8(bank[:, 0:width], m, a, c, width, start=(a == 0))
                 for d in range(0, width, P):
                     add_w4(bank[:, d : d + P], m, a, c + d, P, stop=(a == PASSES - 1 and d == width - P))
-            finish(bank[:, 0:width], m, c, width)
+            relu = work.tile([P, T], F32, name="relu", align_bytes=ALIGN)
+            nc.scalar.activation(out=relu[:, 0:width], in_=bank[:, 0:width], func=ACT.Relu)
+            nc.vector.tensor_tensor(out=last[:, c : c + width], in0=relu[:, 0:width], in1=relu[:, 0:width], op=ALU.mult)
+            if (c + width) % HALF == 0:
+                cols = slice(c + width - HALF, c + width)
+                nc.sync.dma_start(out=out[m * P : (m + 1) * P, cols], in_=last[:, cols])

@@ -24,6 +24,7 @@ BANKS = 8
 ALIGN = 256
 PLANES = 4
 PLANE_COLS = N_OUT // PLANES
+ON_GPSIMD = 3
 EARLY = 4
 LAST_GROUPS = ((0, 256), (256, 128), (384, 128))
 
@@ -54,14 +55,14 @@ def tile_mix_resid_fm_relu2_kernel(tc, x, w4_words, w4_scales, r8_words, r8_scal
                     in_=scales.rearrange("(q r) n -> r q n", r=4)[r].bitcast(I32),
                 )
 
-        def load_packed_scales(queue, planes, scales):
-            for q in range(4):
+        def load_packed_scales(queue, planes, scales, quadrants):
+            for q in quadrants:
                 queue.dma_start(
                     out=planes[32 * q : 32 * q + 4 * PLANES, :].bitcast(I32),
                     in_=scales[4 * q : 4 * q + 4, :].rearrange("r (c n) -> c r n", c=PLANES).bitcast(I32),
                 )
 
-        load_packed_scales(nc.gpsimd, r8_planes[1], r8_scales[1])
+        load_packed_scales(nc.gpsimd, r8_planes[1], r8_scales[1], range(ON_GPSIMD))
 
         x_codes = [keep.tile([P, T], U32, name="x_codes%d" % a, align_bytes=ALIGN) for a in range(PASSES)]
         x_scales = [keep.tile([P, T], U8, name="x_scales%d" % a, align_bytes=ALIGN) for a in range(PASSES)]
@@ -134,7 +135,8 @@ def tile_mix_resid_fm_relu2_kernel(tc, x, w4_words, w4_scales, r8_words, r8_scal
         load_scales(nc.sync, w4_planes[0], 0, w4_scales[0])
         load_w4(0, 0, first)
         load_x(0, HALF, T)
-        load_packed_scales(nc.sync, r8_planes[0], r8_scales[0])
+        load_packed_scales(nc.sync, r8_planes[0], r8_scales[0], range(4))
+        load_packed_scales(nc.sync, r8_planes[1], r8_scales[1], range(ON_GPSIMD, 4))
         load_r8(0, 0, first)
         load_x(1, 0, HALF)
         load_x(1, HALF, T)

@@ -45,7 +45,7 @@ def tile_mix_resid_fm_relu2_kernel(tc, x, w4_words, w4_scales, r8_words, r8_scal
         w4_planes = [keep.tile([P, N_OUT], U8, name="w4_planes%d" % a, align_bytes=ALIGN) for a in range(PASSES)]
         nc.gpsimd.memset(one[:], 0.0)
         nc.scalar.activation(out=one[:], in_=one[:], func=ACT.Relu)
-        for plane in (r8_planes[1], w4_planes[0], r8_planes[0], w4_planes[1]):
+        for plane in (w4_planes[0], r8_planes[1], r8_planes[0], w4_planes[1]):
             nc.vector.memset(plane[:].bitcast(I32), 0)
 
         def load_scales(queue, plane, row0, scales):
@@ -74,12 +74,13 @@ def tile_mix_resid_fm_relu2_kernel(tc, x, w4_words, w4_scales, r8_words, r8_scal
                 out=raw[:],
                 in_=x[a * K_PASS : (a + 1) * K_PASS, c0:c1].rearrange("(p j) w -> p j w", j=PACK),
             )
-            for c in range(c0, c1, HALF):
-                x_raw[(a, c)] = raw[:, :, c - c0 : c - c0 + HALF]
+            x_raw[(a, c0, c1 - c0)] = raw
 
-        def quantize_x(a, c, vec_cols):
-            raw = x_raw[(a, c)]
-            grouped = keep.tile([P, HALF, PACK], BF16, name="x_grouped%d_%d" % (a, c), align_bytes=ALIGN)
+        def quantize_x(a, c, width):
+            raw = x_raw[(a, c, width)]
+            grouped = keep.tile([P, width, PACK], BF16, name="x_grouped%d_%d" % (a, c), align_bytes=ALIGN)
+            step = min(P, width // 2)
+            vec_cols = width * 2 // 3 // 8 * 8
 
             def interleave(copy, c0, c1):
                 copy(
@@ -87,14 +88,14 @@ def tile_mix_resid_fm_relu2_kernel(tc, x, w4_words, w4_scales, r8_words, r8_scal
                     in_=raw[:, :, c0:c1].rearrange("p j (c i) -> p c j i", i=4),
                 )
 
-            interleave(nc.vector.tensor_copy, 0, P)
-            interleave(nc.vector.tensor_copy, P, vec_cols)
-            interleave(nc.scalar.copy, vec_cols, HALF)
-            for d in range(0, HALF, P):
+            interleave(nc.vector.tensor_copy, 0, step)
+            interleave(nc.vector.tensor_copy, step, vec_cols)
+            interleave(nc.scalar.copy, vec_cols, width)
+            for d in range(0, width, step):
                 nc.vector.quantize_mx(
-                    out=x_codes[a][:, c + d : c + d + P].bitcast(E4M3),
-                    scales=x_scales[a][:, c + d : c + d + P],
-                    in_=grouped[:, d : d + P, :].rearrange("p w j -> p (w j)"),
+                    out=x_codes[a][:, c + d : c + d + step].bitcast(E4M3),
+                    scales=x_scales[a][:, c + d : c + d + step],
+                    in_=grouped[:, d : d + step, :].rearrange("p w j -> p (w j)"),
                 )
 
         r8_parts = {}
@@ -131,24 +132,24 @@ def tile_mix_resid_fm_relu2_kernel(tc, x, w4_words, w4_scales, r8_words, r8_scal
                     r8_parts[(a, m)] = r8_rest[:, a, m * P - first : (m + 1) * P - first].bitcast(E4M3)
                     w4_parts[(a, m)] = w4_rest[:, a, 2 * (m * P - first) : 2 * ((m + 1) * P - first)].bitcast(E2M1)
 
-        load_x(0, 0, HALF)
+        load_x(0, 0, P)
         load_scales(nc.sync, w4_planes[0], 0, w4_scales[0])
         load_w4(0, 0, first)
+        load_x(0, P, HALF)
         load_x(0, HALF, T)
         load_packed_scales(nc.sync, r8_planes[0], r8_scales[0], range(4))
         load_packed_scales(nc.sync, r8_planes[1], r8_scales[1], range(ON_GPSIMD, 4))
         load_r8(0, 0, first)
-        load_x(1, 0, HALF)
-        load_x(1, HALF, T)
+        load_x(1, 0, T - P)
         load_r8(1, 0, first // 2)
+        load_x(1, T - P, T)
         load_scales(nc.sync, w4_planes[1], 0, w4_scales[1])
         load_w4(1, 0, first)
         load_r8(1, first // 2, first)
         load_rest()
 
-        for a in range(PASSES):
-            for c in range(0, T, HALF):
-                quantize_x(a, c, 168)
+        for a, c, width in x_raw:
+            quantize_x(a, c, width)
 
         def open_bank(b):
             bank = psum.tile([P, T], F32, name="bank%d" % b)
@@ -193,8 +194,9 @@ def tile_mix_resid_fm_relu2_kernel(tc, x, w4_words, w4_scales, r8_words, r8_scal
             add_r8(banks[m][:], m, 0, 0, T)
         for m in range(EARLY):
             add_r8(banks[m][:, 0:HALF], m, 1, 0, HALF)
-        for m in range(EARLY):
-            add_r8(banks[m][:, HALF:T], m, 1, HALF, HALF)
+        for c in range(HALF, T, P):
+            for m in range(EARLY):
+                add_r8(banks[m][:, c : c + P], m, 1, c, P)
         for m in range(BANKS):
             if m >= EARLY:
                 add_r8(banks[m][:], m, 1, 0, T)

@@ -20,67 +20,65 @@ PACK = 4
 K_PASS = P * PACK
 PASSES = K // K_PASS
 HALF = T // 2
-BANKS = 8
 ALIGN = 256
+N_TILES = N_OUT // P
+BANKS = 8
+PAIRS = BANKS // 2
+FIRST = BANKS * P
 PLANES = 4
 PLANE_COLS = N_OUT // PLANES
-ON_GPSIMD = 3
-EARLY = 4
+EARLY = 5
 LAST_GROUPS = ((0, 256), (256, 128), (384, 128))
 
 
 def tile_mix_resid_fm_relu2_kernel(tc, x, w4_words, w4_scales, r8_words, r8_scales, out):
     nc = tc.nc
-    n_tiles = N_OUT // P
-    first = BANKS * P
 
     with ExitStack() as ctx:
         keep = ctx.enter_context(tc.tile_pool(name="keep", bufs=1))
-        work = ctx.enter_context(tc.tile_pool(name="work", bufs=n_tiles + 3))
+        work = ctx.enter_context(tc.tile_pool(name="work", bufs=N_TILES + 3))
         psum = ctx.enter_context(tc.psum_pool(name="psum", bufs=1))
         ctx.enter_context(tc.manual_schedule())
 
-        one = keep.tile([P, 1], F32, name="one")
-        r8_planes = [keep.tile([P, PLANE_COLS], U8, name="r8_planes%d" % a, align_bytes=ALIGN) for a in range(PASSES)]
         w4_planes = [keep.tile([P, N_OUT], U8, name="w4_planes%d" % a, align_bytes=ALIGN) for a in range(PASSES)]
-        nc.gpsimd.memset(one[:], 0.0)
-        nc.scalar.activation(out=one[:], in_=one[:], func=ACT.Relu)
-        for plane in (w4_planes[0], r8_planes[1], r8_planes[0], w4_planes[1]):
+        r8_planes = [keep.tile([P, PLANE_COLS], U8, name="r8_planes%d" % a, align_bytes=ALIGN) for a in range(PASSES)]
+        for plane in w4_planes + r8_planes:
             nc.vector.memset(plane[:].bitcast(I32), 0)
 
-        def load_scales(queue, plane, row0, scales):
+        def load_w4_scales(queue, a, n0, n1):
             for r in range(4):
                 queue.dma_start(
-                    out=plane[row0 + r : P : 32, :].bitcast(I32),
-                    in_=scales.rearrange("(q r) n -> r q n", r=4)[r].bitcast(I32),
+                    out=w4_planes[a][r:P:32, n0:n1].bitcast(I32),
+                    in_=w4_scales[a].rearrange("(q r) n -> r q n", r=4)[r][:, n0:n1].bitcast(I32),
                 )
 
-        def load_packed_scales(queue, planes, scales, quadrants):
-            for q in quadrants:
-                queue.dma_start(
-                    out=planes[32 * q : 32 * q + 4 * PLANES, :].bitcast(I32),
-                    in_=scales[4 * q : 4 * q + 4, :].rearrange("r (c n) -> c r n", c=PLANES).bitcast(I32),
+        def load_r8_scales(a):
+            for q in range(4):
+                nc.sync.dma_start(
+                    out=r8_planes[a][32 * q : 32 * q + 4 * PLANES, :].bitcast(I32),
+                    in_=r8_scales[a][4 * q : 4 * q + 4, :].rearrange("r (c n) -> c r n", c=PLANES).bitcast(I32),
                 )
 
-        load_packed_scales(nc.gpsimd, r8_planes[1], r8_scales[1], range(ON_GPSIMD))
+        load_w4_scales(nc.gpsimd, 1, 0, N_OUT)
 
         x_codes = [keep.tile([P, T], U32, name="x_codes%d" % a, align_bytes=ALIGN) for a in range(PASSES)]
         x_scales = [keep.tile([P, T], U8, name="x_scales%d" % a, align_bytes=ALIGN) for a in range(PASSES)]
         x_raw = {}
 
-        def load_x(a, c0, c1):
-            raw = keep.tile([P, PACK, c1 - c0], F32, name="x_raw%d_%d" % (a, c0), align_bytes=ALIGN)
+        def load_x(a, c, width):
+            raw = keep.tile([P, PACK, width], F32, name="x_raw%d_%d" % (a, c), align_bytes=ALIGN)
             nc.sync.dma_start(
                 out=raw[:],
-                in_=x[a * K_PASS : (a + 1) * K_PASS, c0:c1].rearrange("(p j) w -> p j w", j=PACK),
+                in_=x[a * K_PASS : (a + 1) * K_PASS, c : c + width].rearrange("(p j) w -> p j w", j=PACK),
             )
-            x_raw[(a, c0, c1 - c0)] = raw
+            x_raw[(a, c)] = raw
 
-        def quantize_x(a, c, width):
-            raw = x_raw[(a, c, width)]
+        def quantize_x(a, c, with_scalar=True):
+            raw = x_raw[(a, c)]
+            width = raw.shape[2]
             grouped = keep.tile([P, width, PACK], BF16, name="x_grouped%d_%d" % (a, c), align_bytes=ALIGN)
-            step = min(P, width // 2)
-            vec_cols = width * 2 // 3 // 8 * 8
+            step = width // 2
+            vec_cols = width * 2 // 3 // 8 * 8 if with_scalar else width
 
             def interleave(copy, c0, c1):
                 copy(
@@ -90,8 +88,9 @@ def tile_mix_resid_fm_relu2_kernel(tc, x, w4_words, w4_scales, r8_words, r8_scal
 
             interleave(nc.vector.tensor_copy, 0, step)
             interleave(nc.vector.tensor_copy, step, vec_cols)
-            interleave(nc.scalar.copy, vec_cols, width)
-            for d in range(0, width, step):
+            if with_scalar:
+                interleave(nc.scalar.copy, vec_cols, width)
+            for d in (0, step):
                 nc.vector.quantize_mx(
                     out=x_codes[a][:, c + d : c + d + step].bitcast(E4M3),
                     scales=x_scales[a][:, c + d : c + d + step],
@@ -101,61 +100,45 @@ def tile_mix_resid_fm_relu2_kernel(tc, x, w4_words, w4_scales, r8_words, r8_scal
         r8_parts = {}
         w4_parts = {}
 
-        def load_r8(a, n0, n1):
-            words = keep.tile([P, n1 - n0], U32, name="r8_%d_%d" % (a, n0), align_bytes=ALIGN)
-            nc.sync.dma_start(
-                out=words[:].bitcast(I32),
-                in_=r8_words[a].rearrange("p n i -> p (n i)")[:, PACK * n0 : PACK * n1].bitcast(I32),
-            )
-            for m in range(n0 // P, n1 // P):
-                r8_parts[(a, m)] = words[:, m * P - n0 : (m + 1) * P - n0].bitcast(E4M3)
+        def load_r8(passes, m0, m1):
+            words = keep.tile([P, len(passes), (m1 - m0) * P], U32, name="r8_%d_%d" % (passes[0], m0), align_bytes=ALIGN)
+            rows = r8_words.rearrange("a p n i -> p a (n i)")[:, passes[0] : passes[-1] + 1, PACK * P * m0 : PACK * P * m1]
+            nc.sync.dma_start(out=words[:].bitcast(I32), in_=rows.bitcast(I32))
+            for i, a in enumerate(passes):
+                for m in range(m0, m1):
+                    r8_parts[(a, m)] = words[:, i, (m - m0) * P : (m - m0 + 1) * P].bitcast(E4M3)
 
-        def load_w4(a, n0, n1):
-            words = keep.tile([P, 2 * (n1 - n0)], U8, name="w4_%d_%d" % (a, n0), align_bytes=ALIGN)
-            nc.sync.dma_start(out=words[:].bitcast(I32), in_=w4_words[a][:, 2 * n0 : 2 * n1].bitcast(I32))
-            for m in range(n0 // P, n1 // P):
-                w4_parts[(a, m)] = words[:, 2 * (m * P - n0) : 2 * ((m + 1) * P - n0)].bitcast(E2M1)
-
-        def load_rest():
-            r8_rest = keep.tile([P, PASSES, N_OUT - first], U32, name="r8_rest", align_bytes=ALIGN)
-            nc.sync.dma_start(
-                out=r8_rest[:].bitcast(I32),
-                in_=r8_words.rearrange("a p n i -> p a (n i)")[:, :, PACK * first :].bitcast(I32),
-            )
-            w4_rest = keep.tile([P, PASSES, 2 * (N_OUT - first)], U8, name="w4_rest", align_bytes=ALIGN)
-            nc.sync.dma_start(
-                out=w4_rest[:].bitcast(I32),
-                in_=w4_words.rearrange("a p n -> p a n")[:, :, 2 * first :].bitcast(I32),
-            )
-            for a in range(PASSES):
-                for m in range(BANKS, n_tiles):
-                    r8_parts[(a, m)] = r8_rest[:, a, m * P - first : (m + 1) * P - first].bitcast(E4M3)
-                    w4_parts[(a, m)] = w4_rest[:, a, 2 * (m * P - first) : 2 * ((m + 1) * P - first)].bitcast(E2M1)
+        def load_w4(passes, m0, m1):
+            words = keep.tile([P, len(passes), 2 * (m1 - m0) * P], U8, name="w4_%d_%d" % (passes[0], m0), align_bytes=ALIGN)
+            rows = w4_words.rearrange("a p n -> p a n")[:, passes[0] : passes[-1] + 1, 2 * P * m0 : 2 * P * m1]
+            nc.sync.dma_start(out=words[:].bitcast(I32), in_=rows.bitcast(I32))
+            for i, a in enumerate(passes):
+                for m in range(m0, m1):
+                    w4_parts[(a, m)] = words[:, i, 2 * (m - m0) * P : 2 * (m - m0 + 1) * P].bitcast(E2M1)
 
         load_x(0, 0, P)
-        load_scales(nc.sync, w4_planes[0], 0, w4_scales[0])
-        load_w4(0, 0, first)
-        load_x(0, P, HALF)
-        load_x(0, HALF, T)
-        load_packed_scales(nc.sync, r8_planes[0], r8_scales[0], range(4))
-        load_packed_scales(nc.sync, r8_planes[1], r8_scales[1], range(ON_GPSIMD, 4))
-        load_r8(0, 0, first)
-        load_x(1, 0, T - P)
-        load_r8(1, 0, first // 2)
-        load_x(1, T - P, T)
-        load_scales(nc.sync, w4_planes[1], 0, w4_scales[1])
-        load_w4(1, 0, first)
-        load_r8(1, first // 2, first)
-        load_rest()
+        load_w4_scales(nc.sync, 0, 0, N_OUT)
+        load_w4((0,), 0, BANKS)
+        for c in range(P, T, P):
+            load_x(0, c, P)
+        load_r8_scales(0)
+        load_r8((0,), 0, BANKS)
+        load_x(1, 0, HALF)
+        load_w4((1,), 0, BANKS)
+        load_r8_scales(1)
+        load_r8((1,), 0, PAIRS)
+        load_x(1, HALF, P)
+        load_r8((1,), PAIRS, BANKS)
+        load_x(1, T - P, P)
+        load_r8((0, 1), BANKS, N_TILES)
+        load_w4((0, 1), BANKS, N_TILES)
 
-        for a, c, width in x_raw:
-            quantize_x(a, c, width)
+        for c in range(0, T, P):
+            quantize_x(0, c)
+        quantize_x(1, 0)
 
-        def open_bank(b):
-            bank = psum.tile([P, T], F32, name="bank%d" % b)
-            return bank
-
-        def add_r8(acc, m, a, c, width, start=False):
+        def add_r8(acc, m, a, c, start=False, stop=False):
+            width = acc.shape[1]
             nc.tensor.matmul_mx(
                 out=acc,
                 lhsT=r8_parts[(a, m)],
@@ -163,10 +146,11 @@ def tile_mix_resid_fm_relu2_kernel(tc, x, w4_words, w4_scales, r8_words, r8_scal
                 rhs=x_codes[a][:, c : c + width].bitcast(E4M3),
                 rhs_scale=x_scales[a][:, c : c + width],
                 start=start,
-                stop=False,
+                stop=stop,
             )
 
-        def add_w4(acc, m, a, c, width, start=False, stop=False):
+        def add_w4(acc, m, a, c, start=False, stop=False):
+            width = acc.shape[1]
             nc.tensor.matmul_mx(
                 out=acc,
                 lhsT=w4_parts[(a, m)],
@@ -177,53 +161,101 @@ def tile_mix_resid_fm_relu2_kernel(tc, x, w4_words, w4_scales, r8_words, r8_scal
                 stop=stop,
             )
 
-        def finish(acc, m, c, width, steps=1):
-            relu = work.tile([P, T], F32, name="relu", align_bytes=ALIGN)
+        def open_bank(b):
+            bank = psum.tile([P, T], F32, name="bank%d" % b)
+            return bank
+
+        def relu(acc):
+            positive = work.tile([P, T], F32, name="positive", align_bytes=ALIGN)
+            view = positive[:, 0 : acc.shape[1]]
+            nc.scalar.activation(out=view, in_=acc, func=ACT.Relu)
+            return view
+
+        def square(result, positive):
+            nc.vector.tensor_tensor(out=result, in0=positive, in1=positive, op=ALU.mult)
+
+        def new_result():
             result = work.tile([P, T], F32, name="result", align_bytes=ALIGN)
-            for d in range(0, width, width // steps):
-                cols = slice(d, d + width // steps)
-                nc.scalar.activation(out=relu[:, cols], in_=acc[:, cols], func=ACT.Relu)
-                nc.vector.tensor_tensor(out=result[:, cols], in0=relu[:, cols], in1=relu[:, cols], op=ALU.mult)
+            return result
+
+        halves = [[open_bank(PAIRS * h + i) for i in range(PAIRS)] for h in range(2)]
+
+        def half_sum(m, c, width):
+            col = m % 2 * HALF + c % HALF
+            return halves[c // HALF][m // 2][:, col : col + width]
+
+        def store_pair(result, i, h):
+            nc.sync.dma_start(
+                out=out[2 * i * P : (2 * i + 2) * P, h * HALF : (h + 1) * HALF].rearrange("(m p) c -> p m c", p=P),
+                in_=result[:].rearrange("p (m c) -> p m c", m=2),
+            )
+
+        def finish_pair(i, h):
+            positive = relu(halves[h][i][:])
+            result = new_result()
+            square(result[:], positive)
+            store_pair(result, i, h)
+
+        def finish(acc, m, c):
+            width = acc.shape[1]
+            positive = relu(acc)
+            result = new_result()
+            square(result[:, 0:width], positive)
             nc.sync.dma_start(out=out[m * P : (m + 1) * P, c : c + width], in_=result[:, 0:width])
 
-        banks = [open_bank(m) for m in range(BANKS)]
         for c in range(0, T, P):
             for m in range(BANKS):
-                add_w4(banks[m][:, c : c + P], m, 0, c, P, start=(c == 0))
+                add_w4(half_sum(m, c, P), m, 0, c, start=(c % HALF == 0 and m % 2 == 0))
         for m in range(BANKS):
-            add_r8(banks[m][:], m, 0, 0, T)
+            for c in (0, HALF):
+                add_r8(half_sum(m, c, HALF), m, 0, c)
+        for m0 in (0, PAIRS):
+            for m in range(m0, m0 + PAIRS):
+                add_w4(half_sum(m, 0, HALF), m, 1, 0)
+            for m in range(m0, m0 + PAIRS):
+                add_r8(half_sum(m, 0, HALF), m, 1, 0, stop=(m % 2 == 1))
+
+        quantize_x(1, HALF, with_scalar=False)
+        positives = [relu(halves[0][i][:]) for i in range(2)]
+        result = new_result()
+        nc.scalar.activation(out=result[:], in_=positives[0], func=ACT.Square)
+        store_pair(result, 0, 0)
+        quantize_x(1, T - P, with_scalar=False)
+        result = new_result()
+        square(result[:], positives[1])
+        store_pair(result, 1, 0)
+        for i in range(2, PAIRS):
+            finish_pair(i, 0)
+
         for m in range(EARLY):
-            add_r8(banks[m][:, 0:HALF], m, 1, 0, HALF)
-        for c in range(HALF, T, P):
-            for m in range(EARLY):
-                add_r8(banks[m][:, c : c + P], m, 1, c, P)
+            add_r8(half_sum(m, HALF, P), m, 1, HALF)
+            add_w4(half_sum(m, HALF, P), m, 1, HALF)
         for m in range(BANKS):
-            if m >= EARLY:
-                add_r8(banks[m][:], m, 1, 0, T)
-            add_w4(banks[m][:], m, 1, 0, T, stop=True)
-            finish(banks[m][:], m, 0, T, steps=2 if m == 0 else 1)
-        for m in range(BANKS, n_tiles - 1):
+            c = T - P if m < EARLY else HALF
+            add_r8(half_sum(m, c, T - c), m, 1, c)
+            add_w4(half_sum(m, c, T - c), m, 1, c, stop=(m % 2 == 1))
+            if m % 2 == 1:
+                finish_pair(m // 2, 1)
+
+        for m in range(BANKS, N_TILES - 1):
             bank = open_bank(m - BANKS)
-            add_r8(bank[:], m, 0, 0, T, start=True)
-            add_w4(bank[:], m, 0, 0, T)
-            add_r8(bank[:], m, 1, 0, T)
-            add_w4(bank[:], m, 1, 0, T, stop=True)
-            if m < n_tiles - 2:
-                finish(bank[:], m, 0, T)
+            for a in range(PASSES):
+                add_r8(bank[:], m, a, 0, start=(a == 0))
+                add_w4(bank[:], m, a, 0, stop=(a == PASSES - 1))
+            if m < N_TILES - 2:
+                finish(bank[:], m, 0)
             else:
-                finish(bank[:, 0:HALF], m, 0, HALF)
-                finish(bank[:, HALF:T], m, HALF, HALF)
-        m = n_tiles - 1
+                finish(bank[:, 0:HALF], m, 0)
+                finish(bank[:, HALF:T], m, HALF)
+
+        m = N_TILES - 1
         last = keep.tile([P, T], F32, name="last", align_bytes=ALIGN)
         for g, (c, width) in enumerate(LAST_GROUPS):
             bank = open_bank(m - BANKS + g)
             for a in range(PASSES):
-                add_r8(bank[:, 0:width], m, a, c, width, start=(a == 0))
-                for d in range(0, width, P):
-                    add_w4(bank[:, d : d + P], m, a, c + d, P, stop=(a == PASSES - 1 and d == width - P))
-            relu = work.tile([P, T], F32, name="relu", align_bytes=ALIGN)
-            nc.scalar.activation(out=relu[:, 0:width], in_=bank[:, 0:width], func=ACT.Relu)
-            nc.vector.tensor_tensor(out=last[:, c : c + width], in0=relu[:, 0:width], in1=relu[:, 0:width], op=ALU.mult)
+                add_r8(bank[:, 0:width], m, a, c, start=(a == 0))
+                add_w4(bank[:, 0:width], m, a, c, stop=(a == PASSES - 1))
+            square(last[:, c : c + width], relu(bank[:, 0:width]))
             if (c + width) % HALF == 0:
                 cols = slice(c + width - HALF, c + width)
                 nc.sync.dma_start(out=out[m * P : (m + 1) * P, cols], in_=last[:, cols])

@@ -28,6 +28,9 @@ FIRST = BANKS * P
 PLANES = 4
 PLANE_COLS = N_OUT // PLANES
 EARLY = 5
+WARM_COLS = 256
+WARM_PASSES = 6
+TWO_ONES = 0x3F803F80
 LAST_GROUPS = ((0, 256), (256, 128), (384, 128))
 
 
@@ -42,8 +45,26 @@ def tile_mix_resid_fm_relu2_kernel(tc, x, w4_words, w4_scales, r8_words, r8_scal
 
         w4_planes = [keep.tile([P, N_OUT], U8, name="w4_planes%d" % a, align_bytes=ALIGN) for a in range(PASSES)]
         r8_planes = [keep.tile([P, PLANE_COLS], U8, name="r8_planes%d" % a, align_bytes=ALIGN) for a in range(PASSES)]
-        for plane in w4_planes + r8_planes:
+        ones = keep.tile([P, PACK * WARM_COLS], BF16, name="ones", align_bytes=ALIGN)
+        ones_codes = keep.tile([P, WARM_COLS], U32, name="ones_codes", align_bytes=ALIGN)
+        ones_scales = keep.tile([P, WARM_COLS], U8, name="ones_scales", align_bytes=ALIGN)
+        nc.vector.memset(w4_planes[0][:].bitcast(I32), 0)
+        nc.vector.memset(ones[:].bitcast(I32), TWO_ONES)
+        nc.vector.memset(w4_planes[1][:].bitcast(I32), 0)
+        nc.vector.quantize_mx(out=ones_codes[:].bitcast(E4M3), scales=ones_scales[:], in_=ones[:])
+        for plane in r8_planes:
             nc.vector.memset(plane[:].bitcast(I32), 0)
+        unread = psum.tile([P, T], F32, name="bank%d" % (BANKS - 1))
+        for turn in range(WARM_PASSES):
+            nc.tensor.matmul_mx(
+                out=unread[:, 0:WARM_COLS],
+                lhsT=ones_codes[:, 0:P].bitcast(E4M3),
+                lhsT_scale=ones_scales[:, 0:P],
+                rhs=ones_codes[:].bitcast(E4M3),
+                rhs_scale=ones_scales[:],
+                start=True,
+                stop=True,
+            )
 
         def load_w4_scales(queue, a, n0, n1):
             for r in range(4):

@@ -25,9 +25,10 @@ N_TILES = N_OUT // P
 BANKS = 8
 PAIRS = BANKS // 2
 FIRST = BANKS * P
+W4_RUNS = ((0, FIRST), (FIRST, N_OUT))
 PLANES = 4
 PLANE_COLS = N_OUT // PLANES
-EARLY = 5
+EARLY = 3
 WARM_COLS = 256
 WARM_PASSES = 6
 TWO_ONES = 0x3F803F80
@@ -43,17 +44,18 @@ def tile_mix_resid_fm_relu2_kernel(tc, x, w4_words, w4_scales, r8_words, r8_scal
         psum = ctx.enter_context(tc.psum_pool(name="psum", bufs=1))
         ctx.enter_context(tc.manual_schedule())
 
-        w4_planes = [keep.tile([P, N_OUT], U8, name="w4_planes%d" % a, align_bytes=ALIGN) for a in range(PASSES)]
+        w4_planes = [
+            keep.tile([P, PASSES, n1 - n0], U8, name="w4_planes%d" % n0, align_bytes=ALIGN) for n0, n1 in W4_RUNS
+        ]
         r8_planes = [keep.tile([P, PLANE_COLS], U8, name="r8_planes%d" % a, align_bytes=ALIGN) for a in range(PASSES)]
         ones = keep.tile([P, PACK * WARM_COLS], BF16, name="ones", align_bytes=ALIGN)
         ones_codes = keep.tile([P, WARM_COLS], U32, name="ones_codes", align_bytes=ALIGN)
         ones_scales = keep.tile([P, WARM_COLS], U8, name="ones_scales", align_bytes=ALIGN)
         nc.vector.memset(w4_planes[0][:].bitcast(I32), 0)
-        nc.vector.memset(ones[:].bitcast(I32), TWO_ONES)
-        nc.vector.memset(w4_planes[1][:].bitcast(I32), 0)
-        nc.vector.quantize_mx(out=ones_codes[:].bitcast(E4M3), scales=ones_scales[:], in_=ones[:])
-        for plane in r8_planes:
+        for plane in r8_planes + w4_planes[1:]:
             nc.vector.memset(plane[:].bitcast(I32), 0)
+        nc.vector.memset(ones[:].bitcast(I32), TWO_ONES)
+        nc.vector.quantize_mx(out=ones_codes[:].bitcast(E4M3), scales=ones_scales[:], in_=ones[:])
         unread = psum.tile([P, T], F32, name="bank%d" % (BANKS - 1))
         for turn in range(WARM_PASSES):
             nc.tensor.matmul_mx(
@@ -66,11 +68,12 @@ def tile_mix_resid_fm_relu2_kernel(tc, x, w4_words, w4_scales, r8_words, r8_scal
                 stop=True,
             )
 
-        def load_w4_scales(queue, a, n0, n1):
+        def load_w4_scales(run):
+            n0, n1 = W4_RUNS[run]
             for r in range(4):
-                queue.dma_start(
-                    out=w4_planes[a][r:P:32, n0:n1].bitcast(I32),
-                    in_=w4_scales[a].rearrange("(q r) n -> r q n", r=4)[r][:, n0:n1].bitcast(I32),
+                nc.sync.dma_start(
+                    out=w4_planes[run][r:P:32, :, :].bitcast(I32),
+                    in_=w4_scales.rearrange("a (q r) n -> r q a n", r=4)[r][:, :, n0:n1].bitcast(I32),
                 )
 
         def load_r8_scales(a):
@@ -80,7 +83,6 @@ def tile_mix_resid_fm_relu2_kernel(tc, x, w4_words, w4_scales, r8_words, r8_scal
                     in_=r8_scales[a][4 * q : 4 * q + 4, :].rearrange("r (c n) -> c r n", c=PLANES).bitcast(I32),
                 )
 
-        load_w4_scales(nc.gpsimd, 1, 0, N_OUT)
 
         x_codes = [keep.tile([P, T], U32, name="x_codes%d" % a, align_bytes=ALIGN) for a in range(PASSES)]
         x_scales = [keep.tile([P, T], U8, name="x_scales%d" % a, align_bytes=ALIGN) for a in range(PASSES)]
@@ -137,10 +139,10 @@ def tile_mix_resid_fm_relu2_kernel(tc, x, w4_words, w4_scales, r8_words, r8_scal
                 for m in range(m0, m1):
                     w4_parts[(a, m)] = words[:, i, 2 * (m - m0) * P : 2 * (m - m0 + 1) * P].bitcast(E2M1)
 
-        load_x(0, 0, P)
-        load_w4_scales(nc.sync, 0, 0, N_OUT)
+        load_x(0, 0, HALF)
+        load_w4_scales(0)
         load_w4((0,), 0, BANKS)
-        for c in range(P, T, P):
+        for c in range(HALF, T, P):
             load_x(0, c, P)
         load_r8_scales(0)
         load_r8((0,), 0, BANKS)
@@ -151,10 +153,11 @@ def tile_mix_resid_fm_relu2_kernel(tc, x, w4_words, w4_scales, r8_words, r8_scal
         load_x(1, HALF, P)
         load_r8((1,), PAIRS, BANKS)
         load_x(1, T - P, P)
+        load_w4_scales(1)
         load_r8((0, 1), BANKS, N_TILES)
         load_w4((0, 1), BANKS, N_TILES)
 
-        for c in range(0, T, P):
+        for c in (0, HALF, T - P):
             quantize_x(0, c)
         quantize_x(1, 0)
 
@@ -175,7 +178,7 @@ def tile_mix_resid_fm_relu2_kernel(tc, x, w4_words, w4_scales, r8_words, r8_scal
             nc.tensor.matmul_mx(
                 out=acc,
                 lhsT=w4_parts[(a, m)],
-                lhsT_scale=w4_planes[a][:, m * P : (m + 1) * P],
+                lhsT_scale=w4_planes[m // BANKS][:, a, m % BANKS * P : (m % BANKS + 1) * P],
                 rhs=x_codes[a][:, c : c + width].bitcast(E4M3),
                 rhs_scale=x_scales[a][:, c : c + width],
                 start=start,
@@ -224,9 +227,9 @@ def tile_mix_resid_fm_relu2_kernel(tc, x, w4_words, w4_scales, r8_words, r8_scal
             square(result[:, 0:width], positive)
             nc.sync.dma_start(out=out[m * P : (m + 1) * P, c : c + width], in_=result[:, 0:width])
 
-        for c in range(0, T, P):
+        for c, width in ((0, HALF), (HALF, P), (T - P, P)):
             for m in range(BANKS):
-                add_w4(half_sum(m, c, P), m, 0, c, start=(c % HALF == 0 and m % 2 == 0))
+                add_w4(half_sum(m, c, width), m, 0, c, start=(c % HALF == 0 and m % 2 == 0))
         for m in range(BANKS):
             for c in (0, HALF):
                 add_r8(half_sum(m, c, HALF), m, 0, c)
@@ -248,12 +251,13 @@ def tile_mix_resid_fm_relu2_kernel(tc, x, w4_words, w4_scales, r8_words, r8_scal
         for i in range(2, PAIRS):
             finish_pair(i, 0)
 
-        for m in range(EARLY):
+        for m in range(BANKS):
             add_r8(half_sum(m, HALF, P), m, 1, HALF)
+        for m in range(EARLY):
             add_w4(half_sum(m, HALF, P), m, 1, HALF)
         for m in range(BANKS):
             c = T - P if m < EARLY else HALF
-            add_r8(half_sum(m, c, T - c), m, 1, c)
+            add_r8(half_sum(m, T - P, P), m, 1, T - P)
             add_w4(half_sum(m, c, T - c), m, 1, c, stop=(m % 2 == 1))
             if m % 2 == 1:
                 finish_pair(m // 2, 1)

@@ -28,9 +28,9 @@ FIRST = BANKS * P
 W4_RUNS = ((0, FIRST), (FIRST, N_OUT))
 PLANES = 4
 PLANE_COLS = N_OUT // PLANES
-EARLY = 3
-WARM_COLS = 256
-WARM_PASSES = 6
+EARLY = 4
+WARM_COLS = 512
+WARM_PASSES = 4
 TWO_ONES = 0x3F803F80
 LAST_GROUPS = ((0, 256), (256, 128), (384, 128))
 
@@ -40,7 +40,7 @@ def tile_mix_resid_fm_relu2_kernel(tc, x, w4_words, w4_scales, r8_words, r8_scal
 
     with ExitStack() as ctx:
         keep = ctx.enter_context(tc.tile_pool(name="keep", bufs=1))
-        work = ctx.enter_context(tc.tile_pool(name="work", bufs=N_TILES + 3))
+        work = ctx.enter_context(tc.tile_pool(name="work", bufs=N_TILES + 4))
         psum = ctx.enter_context(tc.psum_pool(name="psum", bufs=1))
         ctx.enter_context(tc.manual_schedule())
 
@@ -52,10 +52,11 @@ def tile_mix_resid_fm_relu2_kernel(tc, x, w4_words, w4_scales, r8_words, r8_scal
         ones_codes = keep.tile([P, WARM_COLS], U32, name="ones_codes", align_bytes=ALIGN)
         ones_scales = keep.tile([P, WARM_COLS], U8, name="ones_scales", align_bytes=ALIGN)
         nc.vector.memset(w4_planes[0][:].bitcast(I32), 0)
-        for plane in r8_planes + w4_planes[1:]:
-            nc.vector.memset(plane[:].bitcast(I32), 0)
         nc.vector.memset(ones[:].bitcast(I32), TWO_ONES)
+        for plane in r8_planes:
+            nc.vector.memset(plane[:].bitcast(I32), 0)
         nc.vector.quantize_mx(out=ones_codes[:].bitcast(E4M3), scales=ones_scales[:], in_=ones[:])
+        nc.vector.memset(w4_planes[1][:].bitcast(I32), 0)
         unread = psum.tile([P, T], F32, name="bank%d" % (BANKS - 1))
         for turn in range(WARM_PASSES):
             nc.tensor.matmul_mx(
@@ -76,9 +77,9 @@ def tile_mix_resid_fm_relu2_kernel(tc, x, w4_words, w4_scales, r8_words, r8_scal
                     in_=w4_scales.rearrange("a (q r) n -> r q a n", r=4)[r][:, :, n0:n1].bitcast(I32),
                 )
 
-        def load_r8_scales(a):
+        def load_r8_scales(queue, a):
             for q in range(4):
-                nc.sync.dma_start(
+                queue.dma_start(
                     out=r8_planes[a][32 * q : 32 * q + 4 * PLANES, :].bitcast(I32),
                     in_=r8_scales[a][4 * q : 4 * q + 4, :].rearrange("r (c n) -> c r n", c=PLANES).bitcast(I32),
                 )
@@ -142,24 +143,22 @@ def tile_mix_resid_fm_relu2_kernel(tc, x, w4_words, w4_scales, r8_words, r8_scal
         load_x(0, 0, HALF)
         load_w4_scales(0)
         load_w4((0,), 0, BANKS)
-        for c in range(HALF, T, P):
-            load_x(0, c, P)
-        load_r8_scales(0)
+        load_x(0, HALF, P)
+        load_x(0, T - P, P)
         load_r8((0,), 0, BANKS)
+        load_r8_scales(nc.sync, 0)
         load_x(1, 0, HALF)
         load_w4((1,), 0, BANKS)
-        load_r8_scales(1)
+        load_x(1, HALF, HALF)
         load_r8((1,), 0, PAIRS)
-        load_x(1, HALF, P)
+        load_r8_scales(nc.sync, 1)
         load_r8((1,), PAIRS, BANKS)
-        load_x(1, T - P, P)
-        load_w4_scales(1)
         load_r8((0, 1), BANKS, N_TILES)
         load_w4((0, 1), BANKS, N_TILES)
+        load_w4_scales(1)
 
-        for c in (0, HALF, T - P):
-            quantize_x(0, c)
-        quantize_x(1, 0)
+        for a, c in x_raw:
+            quantize_x(a, c)
 
         def add_r8(acc, m, a, c, start=False, stop=False):
             width = acc.shape[1]
@@ -202,65 +201,30 @@ def tile_mix_resid_fm_relu2_kernel(tc, x, w4_words, w4_scales, r8_words, r8_scal
             result = work.tile([P, T], F32, name="result", align_bytes=ALIGN)
             return result
 
-        halves = [[open_bank(PAIRS * h + i) for i in range(PAIRS)] for h in range(2)]
+        banks = [open_bank(m) for m in range(BANKS)]
 
-        def half_sum(m, c, width):
-            col = m % 2 * HALF + c % HALF
-            return halves[c // HALF][m // 2][:, col : col + width]
-
-        def store_pair(result, i, h):
-            nc.sync.dma_start(
-                out=out[2 * i * P : (2 * i + 2) * P, h * HALF : (h + 1) * HALF].rearrange("(m p) c -> p m c", p=P),
-                in_=result[:].rearrange("p (m c) -> p m c", m=2),
-            )
-
-        def finish_pair(i, h):
-            positive = relu(halves[h][i][:])
-            result = new_result()
-            square(result[:], positive)
-            store_pair(result, i, h)
-
-        def finish(acc, m, c):
+        def finish(acc, m, c, steps=1):
             width = acc.shape[1]
-            positive = relu(acc)
             result = new_result()
-            square(result[:, 0:width], positive)
+            for d in range(0, width, width // steps):
+                cols = slice(d, d + width // steps)
+                square(result[:, cols], relu(acc[:, cols]))
             nc.sync.dma_start(out=out[m * P : (m + 1) * P, c : c + width], in_=result[:, 0:width])
 
         for c, width in ((0, HALF), (HALF, P), (T - P, P)):
             for m in range(BANKS):
-                add_w4(half_sum(m, c, width), m, 0, c, start=(c % HALF == 0 and m % 2 == 0))
+                add_w4(banks[m][:, c : c + width], m, 0, c, start=(c == 0))
         for m in range(BANKS):
-            for c in (0, HALF):
-                add_r8(half_sum(m, c, HALF), m, 0, c)
-        for m0 in (0, PAIRS):
-            for m in range(m0, m0 + PAIRS):
-                add_w4(half_sum(m, 0, HALF), m, 1, 0)
-            for m in range(m0, m0 + PAIRS):
-                add_r8(half_sum(m, 0, HALF), m, 1, 0, stop=(m % 2 == 1))
-
-        quantize_x(1, HALF, with_scalar=False)
-        positives = [relu(halves[0][i][:]) for i in range(2)]
-        result = new_result()
-        nc.scalar.activation(out=result[:], in_=positives[0], func=ACT.Square)
-        store_pair(result, 0, 0)
-        quantize_x(1, T - P, with_scalar=False)
-        result = new_result()
-        square(result[:], positives[1])
-        store_pair(result, 1, 0)
-        for i in range(2, PAIRS):
-            finish_pair(i, 0)
-
+            add_r8(banks[m][:], m, 0, 0)
         for m in range(BANKS):
-            add_r8(half_sum(m, HALF, P), m, 1, HALF)
+            add_w4(banks[m][:, 0:HALF], m, 1, 0)
         for m in range(EARLY):
-            add_w4(half_sum(m, HALF, P), m, 1, HALF)
+            add_r8(banks[m][:, 0:HALF], m, 1, 0)
         for m in range(BANKS):
-            c = T - P if m < EARLY else HALF
-            add_r8(half_sum(m, T - P, P), m, 1, T - P)
-            add_w4(half_sum(m, c, T - c), m, 1, c, stop=(m % 2 == 1))
-            if m % 2 == 1:
-                finish_pair(m // 2, 1)
+            c = HALF if m < EARLY else 0
+            add_w4(banks[m][:, HALF:T], m, 1, HALF)
+            add_r8(banks[m][:, c:T], m, 1, c, stop=True)
+            finish(banks[m][:], m, 0, steps=2 if m == 0 else 1)
 
         for m in range(BANKS, N_TILES - 1):
             bank = open_bank(m - BANKS)

@@ -30,7 +30,7 @@ PLANES = 4
 PLANE_COLS = N_OUT // PLANES
 EARLY = 4
 WARM_COLS = 512
-WARM_PASSES = 4
+WARM_WIDTHS = (512, 512, 512, 512, 256)
 TWO_ONES = 0x3F803F80
 LAST_GROUPS = ((0, 256), (256, 128), (384, 128))
 
@@ -52,19 +52,18 @@ def tile_mix_resid_fm_relu2_kernel(tc, x, w4_words, w4_scales, r8_words, r8_scal
         ones_codes = keep.tile([P, WARM_COLS], U32, name="ones_codes", align_bytes=ALIGN)
         ones_scales = keep.tile([P, WARM_COLS], U8, name="ones_scales", align_bytes=ALIGN)
         nc.vector.memset(w4_planes[0][:].bitcast(I32), 0)
-        nc.vector.memset(ones[:].bitcast(I32), TWO_ONES)
-        for plane in r8_planes:
+        for plane in r8_planes + w4_planes[1:]:
             nc.vector.memset(plane[:].bitcast(I32), 0)
+        nc.vector.memset(ones[:].bitcast(I32), TWO_ONES)
         nc.vector.quantize_mx(out=ones_codes[:].bitcast(E4M3), scales=ones_scales[:], in_=ones[:])
-        nc.vector.memset(w4_planes[1][:].bitcast(I32), 0)
         unread = psum.tile([P, T], F32, name="bank%d" % (BANKS - 1))
-        for turn in range(WARM_PASSES):
+        for width in WARM_WIDTHS:
             nc.tensor.matmul_mx(
-                out=unread[:, 0:WARM_COLS],
+                out=unread[:, 0:width],
                 lhsT=ones_codes[:, 0:P].bitcast(E4M3),
                 lhsT_scale=ones_scales[:, 0:P],
-                rhs=ones_codes[:].bitcast(E4M3),
-                rhs_scale=ones_scales[:],
+                rhs=ones_codes[:, 0:width].bitcast(E4M3),
+                rhs_scale=ones_scales[:, 0:width],
                 start=True,
                 stop=True,
             )
@@ -211,9 +210,14 @@ def tile_mix_resid_fm_relu2_kernel(tc, x, w4_words, w4_scales, r8_words, r8_scal
                 square(result[:, cols], relu(acc[:, cols]))
             nc.sync.dma_start(out=out[m * P : (m + 1) * P, c : c + width], in_=result[:, 0:width])
 
-        for c, width in ((0, HALF), (HALF, P), (T - P, P)):
+        for c in (0, P):
+            for m in range(2):
+                add_w4(banks[m][:, c : c + P], m, 0, c, start=(c == 0))
+        for m in range(2, BANKS):
+            add_w4(banks[m][:, 0:HALF], m, 0, 0, start=True)
+        for c in (HALF, T - P):
             for m in range(BANKS):
-                add_w4(banks[m][:, c : c + width], m, 0, c, start=(c == 0))
+                add_w4(banks[m][:, c : c + P], m, 0, c)
         for m in range(BANKS):
             add_r8(banks[m][:], m, 0, 0)
         for m in range(BANKS):
@@ -245,6 +249,4 @@ def tile_mix_resid_fm_relu2_kernel(tc, x, w4_words, w4_scales, r8_words, r8_scal
                 add_r8(bank[:, 0:width], m, a, c, start=(a == 0))
                 add_w4(bank[:, 0:width], m, a, c, stop=(a == PASSES - 1))
             square(last[:, c : c + width], relu(bank[:, 0:width]))
-            if (c + width) % HALF == 0:
-                cols = slice(c + width - HALF, c + width)
-                nc.sync.dma_start(out=out[m * P : (m + 1) * P, cols], in_=last[:, cols])
+            nc.sync.dma_start(out=out[m * P : (m + 1) * P, c : c + width], in_=last[:, c : c + width])

@@ -20,19 +20,20 @@ PACK = 4
 K_PASS = P * PACK
 PASSES = K // K_PASS
 HALF = T // 2
-ALIGN = 256
 N_TILES = N_OUT // P
 BANKS = 8
-PAIRS = BANKS // 2
-FIRST = BANKS * P
-W4_RUNS = ((0, FIRST), (FIRST, N_OUT))
-PLANES = 4
-PLANE_COLS = N_OUT // PLANES
-EARLY = 4
-WARM_COLS = 512
+ALIGN = 256
+QUADRANTS = 4
+W4_RUNS = ((0, BANKS * P), (BANKS * P, N_OUT))
+R8_PLANES = 4
+R8_PLANE_COLS = N_OUT // R8_PLANES
+VECTOR_THIRDS = 2
+STARTERS = 2
+FILLERS = 2
+LAST_GROUPS = ((0, 256), (256, 128), (384, 128))
+RESULTS = N_TILES + 4
 WARM_WIDTHS = (512, 512, 512, 512, 256)
 TWO_ONES = 0x3F803F80
-LAST_GROUPS = ((0, 256), (256, 128), (384, 128))
 
 
 def tile_mix_resid_fm_relu2_kernel(tc, x, w4_words, w4_scales, r8_words, r8_scales, out):
@@ -40,23 +41,29 @@ def tile_mix_resid_fm_relu2_kernel(tc, x, w4_words, w4_scales, r8_words, r8_scal
 
     with ExitStack() as ctx:
         keep = ctx.enter_context(tc.tile_pool(name="keep", bufs=1))
-        work = ctx.enter_context(tc.tile_pool(name="work", bufs=N_TILES + 4))
+        work = ctx.enter_context(tc.tile_pool(name="work", bufs=RESULTS))
         psum = ctx.enter_context(tc.psum_pool(name="psum", bufs=1))
         ctx.enter_context(tc.manual_schedule())
+
+        def open_bank(b):
+            bank = psum.tile([P, T], F32, name="bank%d" % b)
+            return bank
 
         w4_planes = [
             keep.tile([P, PASSES, n1 - n0], U8, name="w4_planes%d" % n0, align_bytes=ALIGN) for n0, n1 in W4_RUNS
         ]
-        r8_planes = [keep.tile([P, PLANE_COLS], U8, name="r8_planes%d" % a, align_bytes=ALIGN) for a in range(PASSES)]
-        ones = keep.tile([P, PACK * WARM_COLS], BF16, name="ones", align_bytes=ALIGN)
-        ones_codes = keep.tile([P, WARM_COLS], U32, name="ones_codes", align_bytes=ALIGN)
-        ones_scales = keep.tile([P, WARM_COLS], U8, name="ones_scales", align_bytes=ALIGN)
-        nc.vector.memset(w4_planes[0][:].bitcast(I32), 0)
-        for plane in r8_planes + w4_planes[1:]:
+        r8_planes = [keep.tile([P, R8_PLANE_COLS], U8, name="r8_planes%d" % a, align_bytes=ALIGN) for a in range(PASSES)]
+        ones = keep.tile([P, PACK * HALF], BF16, name="ones", align_bytes=ALIGN)
+        ones_codes = keep.tile([P, T], U32, name="ones_codes", align_bytes=ALIGN)
+        ones_scales = keep.tile([P, T], U8, name="ones_scales", align_bytes=ALIGN)
+        for plane in w4_planes[:1] + r8_planes + w4_planes[1:]:
             nc.vector.memset(plane[:].bitcast(I32), 0)
+
         nc.vector.memset(ones[:].bitcast(I32), TWO_ONES)
-        nc.vector.quantize_mx(out=ones_codes[:].bitcast(E4M3), scales=ones_scales[:], in_=ones[:])
-        unread = psum.tile([P, T], F32, name="bank%d" % (BANKS - 1))
+        for c in (0, HALF):
+            cols = slice(c, c + HALF)
+            nc.vector.quantize_mx(out=ones_codes[:, cols].bitcast(E4M3), scales=ones_scales[:, cols], in_=ones[:])
+        unread = open_bank(BANKS - 1)
         for width in WARM_WIDTHS:
             nc.tensor.matmul_mx(
                 out=unread[:, 0:width],
@@ -76,13 +83,12 @@ def tile_mix_resid_fm_relu2_kernel(tc, x, w4_words, w4_scales, r8_words, r8_scal
                     in_=w4_scales.rearrange("a (q r) n -> r q a n", r=4)[r][:, :, n0:n1].bitcast(I32),
                 )
 
-        def load_r8_scales(queue, a):
-            for q in range(4):
-                queue.dma_start(
-                    out=r8_planes[a][32 * q : 32 * q + 4 * PLANES, :].bitcast(I32),
-                    in_=r8_scales[a][4 * q : 4 * q + 4, :].rearrange("r (c n) -> c r n", c=PLANES).bitcast(I32),
+        def load_r8_scales(a):
+            for q in range(QUADRANTS):
+                nc.sync.dma_start(
+                    out=r8_planes[a][32 * q : 32 * q + 4 * R8_PLANES, :].bitcast(I32),
+                    in_=r8_scales[a][4 * q : 4 * q + 4, :].rearrange("r (c n) -> c r n", c=R8_PLANES).bitcast(I32),
                 )
-
 
         x_codes = [keep.tile([P, T], U32, name="x_codes%d" % a, align_bytes=ALIGN) for a in range(PASSES)]
         x_scales = [keep.tile([P, T], U8, name="x_scales%d" % a, align_bytes=ALIGN) for a in range(PASSES)]
@@ -96,12 +102,12 @@ def tile_mix_resid_fm_relu2_kernel(tc, x, w4_words, w4_scales, r8_words, r8_scal
             )
             x_raw[(a, c)] = raw
 
-        def quantize_x(a, c, with_scalar=True):
+        def quantize_x(a, c):
             raw = x_raw[(a, c)]
             width = raw.shape[2]
             grouped = keep.tile([P, width, PACK], BF16, name="x_grouped%d_%d" % (a, c), align_bytes=ALIGN)
             step = width // 2
-            vec_cols = width * 2 // 3 // 8 * 8 if with_scalar else width
+            vector_cols = width * VECTOR_THIRDS // 3 // 8 * 8
 
             def interleave(copy, c0, c1):
                 copy(
@@ -110,9 +116,8 @@ def tile_mix_resid_fm_relu2_kernel(tc, x, w4_words, w4_scales, r8_words, r8_scal
                 )
 
             interleave(nc.vector.tensor_copy, 0, step)
-            interleave(nc.vector.tensor_copy, step, vec_cols)
-            if with_scalar:
-                interleave(nc.scalar.copy, vec_cols, width)
+            interleave(nc.vector.tensor_copy, step, vector_cols)
+            interleave(nc.scalar.copy, vector_cols, width)
             for d in (0, step):
                 nc.vector.quantize_mx(
                     out=x_codes[a][:, c + d : c + d + step].bitcast(E4M3),
@@ -145,13 +150,13 @@ def tile_mix_resid_fm_relu2_kernel(tc, x, w4_words, w4_scales, r8_words, r8_scal
         load_x(0, HALF, P)
         load_x(0, T - P, P)
         load_r8((0,), 0, BANKS)
-        load_r8_scales(nc.sync, 0)
+        load_r8_scales(0)
         load_x(1, 0, HALF)
         load_w4((1,), 0, BANKS)
         load_x(1, HALF, HALF)
-        load_r8((1,), 0, PAIRS)
-        load_r8_scales(nc.sync, 1)
-        load_r8((1,), PAIRS, BANKS)
+        load_r8((1,), 0, BANKS // 2)
+        load_r8_scales(1)
+        load_r8((1,), BANKS // 2, BANKS)
         load_r8((0, 1), BANKS, N_TILES)
         load_w4((0, 1), BANKS, N_TILES)
         load_w4_scales(1)
@@ -161,10 +166,11 @@ def tile_mix_resid_fm_relu2_kernel(tc, x, w4_words, w4_scales, r8_words, r8_scal
 
         def add_r8(acc, m, a, c, start=False, stop=False):
             width = acc.shape[1]
+            plane, col = divmod(m * P, R8_PLANE_COLS)
             nc.tensor.matmul_mx(
                 out=acc,
                 lhsT=r8_parts[(a, m)],
-                lhsT_scale=r8_planes[a][4 * (m * P // PLANE_COLS) :, m * P % PLANE_COLS : m * P % PLANE_COLS + P],
+                lhsT_scale=r8_planes[a][4 * plane :, col : col + P],
                 rhs=x_codes[a][:, c : c + width].bitcast(E4M3),
                 rhs_scale=x_scales[a][:, c : c + width],
                 start=start,
@@ -173,62 +179,78 @@ def tile_mix_resid_fm_relu2_kernel(tc, x, w4_words, w4_scales, r8_words, r8_scal
 
         def add_w4(acc, m, a, c, start=False, stop=False):
             width = acc.shape[1]
+            run, place = divmod(m, BANKS)
             nc.tensor.matmul_mx(
                 out=acc,
                 lhsT=w4_parts[(a, m)],
-                lhsT_scale=w4_planes[m // BANKS][:, a, m % BANKS * P : (m % BANKS + 1) * P],
+                lhsT_scale=w4_planes[run][:, a, place * P : (place + 1) * P],
                 rhs=x_codes[a][:, c : c + width].bitcast(E4M3),
                 rhs_scale=x_scales[a][:, c : c + width],
                 start=start,
                 stop=stop,
             )
 
-        def open_bank(b):
-            bank = psum.tile([P, T], F32, name="bank%d" % b)
-            return bank
-
-        def relu(acc):
+        def relu_square(result, acc):
             positive = work.tile([P, T], F32, name="positive", align_bytes=ALIGN)
             view = positive[:, 0 : acc.shape[1]]
             nc.scalar.activation(out=view, in_=acc, func=ACT.Relu)
-            return view
-
-        def square(result, positive):
-            nc.vector.tensor_tensor(out=result, in0=positive, in1=positive, op=ALU.mult)
-
-        def new_result():
-            result = work.tile([P, T], F32, name="result", align_bytes=ALIGN)
-            return result
-
-        banks = [open_bank(m) for m in range(BANKS)]
+            nc.vector.tensor_tensor(out=result, in0=view, in1=view, op=ALU.mult)
 
         def finish(acc, m, c, steps=1):
             width = acc.shape[1]
-            result = new_result()
+            result = work.tile([P, T], F32, name="result", align_bytes=ALIGN)
             for d in range(0, width, width // steps):
                 cols = slice(d, d + width // steps)
-                square(result[:, cols], relu(acc[:, cols]))
+                relu_square(result[:, cols], acc[:, cols])
             nc.sync.dma_start(out=out[m * P : (m + 1) * P, c : c + width], in_=result[:, 0:width])
 
+        banks = [open_bank(m) for m in range(BANKS)]
+
+        def place(m, c, width):
+            if m < 2:
+                col = m * HALF + c % HALF
+                return banks[c // HALF][:, col : col + width]
+            return banks[m][:, c : c + width]
+
+        def finish_pair(h, steps=1):
+            result = work.tile([P, T], F32, name="result", align_bytes=ALIGN)
+            for d in range(0, T, T // steps):
+                cols = slice(d, d + T // steps)
+                relu_square(result[:, cols], banks[h][:, cols])
+            nc.sync.dma_start(
+                out=out[0 : 2 * P, h * HALF : (h + 1) * HALF].rearrange("(m p) c -> p m c", p=P),
+                in_=result[:].rearrange("p (m c) -> p m c", m=2),
+            )
+
         for c in (0, P):
-            for m in range(2):
-                add_w4(banks[m][:, c : c + P], m, 0, c, start=(c == 0))
-        for m in range(2, BANKS):
-            add_w4(banks[m][:, 0:HALF], m, 0, 0, start=True)
+            for m in range(STARTERS):
+                add_w4(place(m, c, P), m, 0, c, start=(c == 0 and m == 0))
+        for m in range(STARTERS, BANKS):
+            add_w4(place(m, 0, HALF), m, 0, 0, start=True)
         for c in (HALF, T - P):
             for m in range(BANKS):
-                add_w4(banks[m][:, c : c + P], m, 0, c)
-        for m in range(BANKS):
+                add_w4(place(m, c, P), m, 0, c, start=(c == HALF and m == 0))
+        for m in range(2):
+            for c in (0, HALF):
+                add_r8(place(m, c, HALF), m, 0, c)
+        for m in range(2, BANKS):
             add_r8(banks[m][:], m, 0, 0)
-        for m in range(BANKS):
-            add_w4(banks[m][:, 0:HALF], m, 1, 0)
-        for m in range(EARLY):
-            add_r8(banks[m][:, 0:HALF], m, 1, 0)
-        for m in range(BANKS):
-            c = HALF if m < EARLY else 0
+
+        for m in range(8):
+            add_w4(place(m, 0, HALF), m, 1, 0)
+        for m in range(2):
+            add_r8(place(m, 0, HALF), m, 1, 0, stop=(m == 1))
+        finish_pair(0, steps=2)
+        for m in range(8, BANKS):
+            add_w4(place(m, 0, HALF), m, 1, 0)
+        for m in range(2):
+            add_w4(place(m, HALF, HALF), m, 1, HALF)
+            add_r8(place(m, HALF, HALF), m, 1, HALF, stop=(m == 1))
+        finish_pair(1)
+        for m in range(2, BANKS):
             add_w4(banks[m][:, HALF:T], m, 1, HALF)
-            add_r8(banks[m][:, c:T], m, 1, c, stop=True)
-            finish(banks[m][:], m, 0, steps=2 if m == 0 else 1)
+            add_r8(banks[m][:], m, 1, 0, stop=True)
+            finish(banks[m][:], m, 0)
 
         for m in range(BANKS, N_TILES - 1):
             bank = open_bank(m - BANKS)
@@ -248,5 +270,7 @@ def tile_mix_resid_fm_relu2_kernel(tc, x, w4_words, w4_scales, r8_words, r8_scal
             for a in range(PASSES):
                 add_r8(bank[:, 0:width], m, a, c, start=(a == 0))
                 add_w4(bank[:, 0:width], m, a, c, stop=(a == PASSES - 1))
-            square(last[:, c : c + width], relu(bank[:, 0:width]))
-            nc.sync.dma_start(out=out[m * P : (m + 1) * P, c : c + width], in_=last[:, c : c + width])
+            relu_square(last[:, c : c + width], bank[:, 0:width])
+            if (c + width) % HALF == 0:
+                cols = slice(c + width - HALF, c + width)
+                nc.sync.dma_start(out=out[m * P : (m + 1) * P, cols], in_=last[:, cols])

@@ -28,8 +28,7 @@ W4_RUNS = ((0, BANKS * P), (BANKS * P, N_OUT))
 R8_PLANES = 4
 R8_PLANE_COLS = N_OUT // R8_PLANES
 VECTOR_THIRDS = 2
-STARTERS = 2
-FILLERS = 2
+HALVED = 2
 LAST_GROUPS = ((0, 256), (256, 128), (384, 128))
 RESULTS = N_TILES + 4
 WARM_WIDTHS = (512, 512, 512, 512, 256)
@@ -190,64 +189,64 @@ def tile_mix_resid_fm_relu2_kernel(tc, x, w4_words, w4_scales, r8_words, r8_scal
                 stop=stop,
             )
 
-        def relu_square(result, acc):
+        def relu(acc):
             positive = work.tile([P, T], F32, name="positive", align_bytes=ALIGN)
             view = positive[:, 0 : acc.shape[1]]
             nc.scalar.activation(out=view, in_=acc, func=ACT.Relu)
-            nc.vector.tensor_tensor(out=result, in0=view, in1=view, op=ALU.mult)
+            return view
 
-        def finish(acc, m, c, steps=1):
+        def relu_square(result, acc):
+            positive = relu(acc)
+            nc.vector.tensor_tensor(out=result, in0=positive, in1=positive, op=ALU.mult)
+
+        def finish(acc, m, c):
             width = acc.shape[1]
             result = work.tile([P, T], F32, name="result", align_bytes=ALIGN)
-            for d in range(0, width, width // steps):
-                cols = slice(d, d + width // steps)
-                relu_square(result[:, cols], acc[:, cols])
+            relu_square(result[:, 0:width], acc)
             nc.sync.dma_start(out=out[m * P : (m + 1) * P, c : c + width], in_=result[:, 0:width])
 
         banks = [open_bank(m) for m in range(BANKS)]
 
         def place(m, c, width):
-            if m < 2:
+            if m < HALVED:
                 col = m * HALF + c % HALF
                 return banks[c // HALF][:, col : col + width]
             return banks[m][:, c : c + width]
 
-        def finish_pair(h, steps=1):
+        def finish_halves(h, steps=1):
             result = work.tile([P, T], F32, name="result", align_bytes=ALIGN)
             for d in range(0, T, T // steps):
                 cols = slice(d, d + T // steps)
                 relu_square(result[:, cols], banks[h][:, cols])
             nc.sync.dma_start(
-                out=out[0 : 2 * P, h * HALF : (h + 1) * HALF].rearrange("(m p) c -> p m c", p=P),
-                in_=result[:].rearrange("p (m c) -> p m c", m=2),
+                out=out[0 : HALVED * P, h * HALF : (h + 1) * HALF].rearrange("(m p) c -> p m c", p=P),
+                in_=result[:].rearrange("p (m c) -> p m c", m=HALVED),
             )
 
         for c in (0, P):
-            for m in range(STARTERS):
+            for m in range(HALVED):
                 add_w4(place(m, c, P), m, 0, c, start=(c == 0 and m == 0))
-        for m in range(STARTERS, BANKS):
+        for m in range(HALVED, BANKS):
             add_w4(place(m, 0, HALF), m, 0, 0, start=True)
         for c in (HALF, T - P):
             for m in range(BANKS):
                 add_w4(place(m, c, P), m, 0, c, start=(c == HALF and m == 0))
-        for m in range(2):
+        for m in range(HALVED):
             for c in (0, HALF):
                 add_r8(place(m, c, HALF), m, 0, c)
-        for m in range(2, BANKS):
+        for m in range(HALVED, BANKS):
             add_r8(banks[m][:], m, 0, 0)
 
-        for m in range(8):
+        for m in range(BANKS):
             add_w4(place(m, 0, HALF), m, 1, 0)
-        for m in range(2):
-            add_r8(place(m, 0, HALF), m, 1, 0, stop=(m == 1))
-        finish_pair(0, steps=2)
-        for m in range(8, BANKS):
-            add_w4(place(m, 0, HALF), m, 1, 0)
-        for m in range(2):
+        for m in range(HALVED):
+            add_r8(place(m, 0, HALF), m, 1, 0, stop=(m == HALVED - 1))
+        finish_halves(0, steps=2)
+        for m in range(HALVED):
             add_w4(place(m, HALF, HALF), m, 1, HALF)
-            add_r8(place(m, HALF, HALF), m, 1, HALF, stop=(m == 1))
-        finish_pair(1)
-        for m in range(2, BANKS):
+            add_r8(place(m, HALF, HALF), m, 1, HALF, stop=(m == HALVED - 1))
+        finish_halves(1)
+        for m in range(HALVED, BANKS):
             add_w4(banks[m][:, HALF:T], m, 1, HALF)
             add_r8(banks[m][:], m, 1, 0, stop=True)
             finish(banks[m][:], m, 0)
@@ -270,7 +269,10 @@ def tile_mix_resid_fm_relu2_kernel(tc, x, w4_words, w4_scales, r8_words, r8_scal
             for a in range(PASSES):
                 add_r8(bank[:, 0:width], m, a, c, start=(a == 0))
                 add_w4(bank[:, 0:width], m, a, c, stop=(a == PASSES - 1))
-            relu_square(last[:, c : c + width], bank[:, 0:width])
+            if c + width < T:
+                relu_square(last[:, c : c + width], bank[:, 0:width])
+            else:
+                nc.scalar.activation(out=last[:, c:T], in_=relu(bank[:, 0:width]), func=ACT.Square)
             if (c + width) % HALF == 0:
                 cols = slice(c + width - HALF, c + width)
                 nc.sync.dma_start(out=out[m * P : (m + 1) * P, cols], in_=last[:, cols])

@@ -189,21 +189,26 @@ def tile_mix_resid_fm_relu2_kernel(tc, x, w4_words, w4_scales, r8_words, r8_scal
                 stop=stop,
             )
 
-        def relu(acc):
+        def positive_like(acc):
             positive = work.tile([P, T], F32, name="positive", align_bytes=ALIGN)
-            view = positive[:, 0 : acc.shape[1]]
-            nc.scalar.activation(out=view, in_=acc, func=ACT.Relu)
-            return view
+            return positive[:, 0 : acc.shape[1]]
 
-        def relu_square(result, acc):
-            positive = relu(acc)
+        def relu_on_scalar(acc):
+            positive = positive_like(acc)
+            nc.scalar.activation(out=positive, in_=acc, func=ACT.Relu)
+            return positive
+
+        def square_on_vector(result, positive):
             nc.vector.tensor_tensor(out=result, in0=positive, in1=positive, op=ALU.mult)
+
+        def square_on_scalar(result, positive):
+            nc.scalar.activation(out=result, in_=positive, func=ACT.Square)
 
         def finish(acc, m, c):
             width = acc.shape[1]
-            result = work.tile([P, T], F32, name="result", align_bytes=ALIGN)
-            relu_square(result[:, 0:width], acc)
-            nc.sync.dma_start(out=out[m * P : (m + 1) * P, c : c + width], in_=result[:, 0:width])
+            result = keep.tile([P, width], F32, name="result%d_%d" % (m, c), align_bytes=ALIGN)
+            square_on_vector(result[:], relu_on_scalar(acc))
+            nc.sync.dma_start(out=out[m * P : (m + 1) * P, c : c + width], in_=result[:])
 
         banks = [open_bank(m) for m in range(BANKS)]
 
@@ -214,10 +219,10 @@ def tile_mix_resid_fm_relu2_kernel(tc, x, w4_words, w4_scales, r8_words, r8_scal
             return banks[m][:, c : c + width]
 
         def finish_halves(h, steps=1):
-            result = work.tile([P, T], F32, name="result", align_bytes=ALIGN)
+            result = keep.tile([P, T], F32, name="halves%d" % h, align_bytes=ALIGN)
             for d in range(0, T, T // steps):
                 cols = slice(d, d + T // steps)
-                relu_square(result[:, cols], banks[h][:, cols])
+                square_on_vector(result[:, cols], relu_on_scalar(banks[h][:, cols]))
             nc.sync.dma_start(
                 out=out[0 : HALVED * P, h * HALF : (h + 1) * HALF].rearrange("(m p) c -> p m c", p=P),
                 in_=result[:].rearrange("p (m c) -> p m c", m=HALVED),
@@ -246,10 +251,13 @@ def tile_mix_resid_fm_relu2_kernel(tc, x, w4_words, w4_scales, r8_words, r8_scal
             add_w4(place(m, HALF, HALF), m, 1, HALF)
             add_r8(place(m, HALF, HALF), m, 1, HALF, stop=(m == HALVED - 1))
         finish_halves(1)
-        for m in range(HALVED, BANKS):
-            add_w4(banks[m][:, HALF:T], m, 1, HALF)
-            add_r8(banks[m][:], m, 1, 0, stop=True)
-            finish(banks[m][:], m, 0)
+        for m0 in range(HALVED, BANKS, 2):
+            pair = keep.tile([P, 2, T], F32, name="pair%d" % m0, align_bytes=ALIGN)
+            for m in (m0, m0 + 1):
+                add_w4(banks[m][:, HALF:T], m, 1, HALF)
+                add_r8(banks[m][:], m, 1, 0, stop=True)
+                square_on_vector(pair[:, m - m0, :], relu_on_scalar(banks[m][:]))
+            nc.sync.dma_start(out=out[m0 * P : (m0 + 2) * P, :].rearrange("(m p) c -> p m c", p=P), in_=pair[:])
 
         for m in range(BANKS, N_TILES - 1):
             bank = open_bank(m - BANKS)
@@ -270,9 +278,9 @@ def tile_mix_resid_fm_relu2_kernel(tc, x, w4_words, w4_scales, r8_words, r8_scal
                 add_r8(bank[:, 0:width], m, a, c, start=(a == 0))
                 add_w4(bank[:, 0:width], m, a, c, stop=(a == PASSES - 1))
             if c + width < T:
-                relu_square(last[:, c : c + width], bank[:, 0:width])
+                square_on_vector(last[:, c : c + width], relu_on_scalar(bank[:, 0:width]))
             else:
-                nc.scalar.activation(out=last[:, c:T], in_=relu(bank[:, 0:width]), func=ACT.Square)
+                square_on_scalar(last[:, c:T], relu_on_scalar(bank[:, 0:width]))
             if (c + width) % HALF == 0:
                 cols = slice(c + width - HALF, c + width)
                 nc.sync.dma_start(out=out[m * P : (m + 1) * P, cols], in_=last[:, cols])

@@ -189,25 +189,19 @@ def tile_mix_resid_fm_relu2_kernel(tc, x, w4_words, w4_scales, r8_words, r8_scal
                 stop=stop,
             )
 
-        def positive_like(acc):
-            positive = work.tile([P, T], F32, name="positive", align_bytes=ALIGN)
-            return positive[:, 0 : acc.shape[1]]
+        def buffer_like(acc):
+            sums = work.tile([P, T], F32, name="sums", align_bytes=ALIGN)
+            return sums[:, 0 : acc.shape[1]]
 
-        def relu_on_scalar(acc):
-            positive = positive_like(acc)
-            nc.scalar.activation(out=positive, in_=acc, func=ACT.Relu)
-            return positive
-
-        def square_on_vector(result, positive):
-            nc.vector.tensor_tensor(out=result, in0=positive, in1=positive, op=ALU.mult)
-
-        def square_on_scalar(result, positive):
-            nc.scalar.activation(out=result, in_=positive, func=ACT.Square)
+        def relu_square(result, acc):
+            sums = buffer_like(acc)
+            nc.scalar.copy(out=sums, in_=acc)
+            nc.vector.scalar_tensor_tensor(out=result, in0=sums, scalar=0.0, in1=sums, op0=ALU.max, op1=ALU.mult)
 
         def finish(acc, m, c):
             width = acc.shape[1]
             result = keep.tile([P, width], F32, name="result%d_%d" % (m, c), align_bytes=ALIGN)
-            square_on_vector(result[:], relu_on_scalar(acc))
+            relu_square(result[:], acc)
             nc.sync.dma_start(out=out[m * P : (m + 1) * P, c : c + width], in_=result[:])
 
         banks = [open_bank(m) for m in range(BANKS)]
@@ -222,7 +216,7 @@ def tile_mix_resid_fm_relu2_kernel(tc, x, w4_words, w4_scales, r8_words, r8_scal
             result = keep.tile([P, T], F32, name="halves%d" % h, align_bytes=ALIGN)
             for d in range(0, T, T // steps):
                 cols = slice(d, d + T // steps)
-                square_on_vector(result[:, cols], relu_on_scalar(banks[h][:, cols]))
+                relu_square(result[:, cols], banks[h][:, cols])
             nc.sync.dma_start(
                 out=out[0 : HALVED * P, h * HALF : (h + 1) * HALF].rearrange("(m p) c -> p m c", p=P),
                 in_=result[:].rearrange("p (m c) -> p m c", m=HALVED),
@@ -256,7 +250,7 @@ def tile_mix_resid_fm_relu2_kernel(tc, x, w4_words, w4_scales, r8_words, r8_scal
             for m in (m0, m0 + 1):
                 add_w4(banks[m][:, HALF:T], m, 1, HALF)
                 add_r8(banks[m][:], m, 1, 0, stop=True)
-                square_on_vector(pair[:, m - m0, :], relu_on_scalar(banks[m][:]))
+                relu_square(pair[:, m - m0, :], banks[m][:])
             nc.sync.dma_start(out=out[m0 * P : (m0 + 2) * P, :].rearrange("(m p) c -> p m c", p=P), in_=pair[:])
 
         for m in range(BANKS, N_TILES - 1):
@@ -278,9 +272,11 @@ def tile_mix_resid_fm_relu2_kernel(tc, x, w4_words, w4_scales, r8_words, r8_scal
                 add_r8(bank[:, 0:width], m, a, c, start=(a == 0))
                 add_w4(bank[:, 0:width], m, a, c, stop=(a == PASSES - 1))
             if c + width < T:
-                square_on_vector(last[:, c : c + width], relu_on_scalar(bank[:, 0:width]))
+                relu_square(last[:, c : c + width], bank[:, 0:width])
             else:
-                square_on_scalar(last[:, c:T], relu_on_scalar(bank[:, 0:width]))
+                positive = buffer_like(bank[:, 0:width])
+                nc.scalar.activation(out=positive, in_=bank[:, 0:width], func=ACT.Relu)
+                nc.scalar.activation(out=last[:, c:T], in_=positive, func=ACT.Square)
             if (c + width) % HALF == 0:
                 cols = slice(c + width - HALF, c + width)
                 nc.sync.dma_start(out=out[m * P : (m + 1) * P, cols], in_=last[:, cols])

@@ -27,7 +27,8 @@ QUADRANTS = 4
 W4_RUNS = ((0, BANKS * P), (BANKS * P, N_OUT))
 R8_PLANES = 4
 R8_PLANE_COLS = N_OUT // R8_PLANES
-VECTOR_THIRDS = 2
+VECTOR_COLS = {P: 64, HALF: 144}
+FIRST_VECTOR_COLS = 168
 HALVED = 2
 LAST_GROUPS = ((0, 256), (256, 128), (384, 128))
 RESULTS = N_TILES + 4
@@ -105,8 +106,6 @@ def tile_mix_resid_fm_relu2_kernel(tc, x, w4_words, w4_scales, r8_words, r8_scal
             raw = x_raw[(a, c)]
             width = raw.shape[2]
             grouped = keep.tile([P, width, PACK], BF16, name="x_grouped%d_%d" % (a, c), align_bytes=ALIGN)
-            step = width // 2
-            vector_cols = width * VECTOR_THIRDS // 3 // 8 * 8
 
             def interleave(copy, c0, c1):
                 copy(
@@ -114,10 +113,16 @@ def tile_mix_resid_fm_relu2_kernel(tc, x, w4_words, w4_scales, r8_words, r8_scal
                     in_=raw[:, :, c0:c1].rearrange("p j (c i) -> p c j i", i=4),
                 )
 
-            interleave(nc.vector.tensor_copy, 0, step)
-            interleave(nc.vector.tensor_copy, step, vector_cols)
-            interleave(nc.scalar.copy, vector_cols, width)
-            for d in (0, step):
+            if (a, c) == (0, 0):
+                step = P
+                interleave(nc.vector.tensor_copy, 0, P)
+                interleave(nc.vector.tensor_copy, P, FIRST_VECTOR_COLS)
+                interleave(nc.scalar.copy, FIRST_VECTOR_COLS, width)
+            else:
+                step = width
+                interleave(nc.vector.tensor_copy, 0, VECTOR_COLS[width])
+                interleave(nc.scalar.copy, VECTOR_COLS[width], width)
+            for d in range(0, width, step):
                 nc.vector.quantize_mx(
                     out=x_codes[a][:, c + d : c + d + step].bitcast(E4M3),
                     scales=x_scales[a][:, c + d : c + d + step],

@@ -32,7 +32,7 @@ FIRST_VECTOR_COLS = 168
 HALVED = 2
 LAST_GROUPS = ((0, 256), (256, 128), (384, 128))
 RESULTS = N_TILES + 4
-WARM_WIDTHS = (512, 512, 512, 512, 256)
+WARM_WIDTHS = (256, 512, 512, 512, 512)
 TWO_ONES = 0x3F803F80
 
 
@@ -56,13 +56,14 @@ def tile_mix_resid_fm_relu2_kernel(tc, x, w4_words, w4_scales, r8_words, r8_scal
         ones = keep.tile([P, PACK * HALF], BF16, name="ones", align_bytes=ALIGN)
         ones_codes = keep.tile([P, T], U32, name="ones_codes", align_bytes=ALIGN)
         ones_scales = keep.tile([P, T], U8, name="ones_scales", align_bytes=ALIGN)
-        for plane in w4_planes[:1] + r8_planes + w4_planes[1:]:
-            nc.vector.memset(plane[:].bitcast(I32), 0)
+        nc.vector.memset(w4_planes[0][:].bitcast(I32), 0)
 
         nc.vector.memset(ones[:].bitcast(I32), TWO_ONES)
         for c in (0, HALF):
             cols = slice(c, c + HALF)
             nc.vector.quantize_mx(out=ones_codes[:, cols].bitcast(E4M3), scales=ones_scales[:, cols], in_=ones[:])
+        for plane in r8_planes + w4_planes[1:]:
+            nc.vector.memset(plane[:].bitcast(I32), 0)
         unread = open_bank(BANKS - 1)
         for width in WARM_WIDTHS:
             nc.tensor.matmul_mx(

@@ -256,6 +256,7 @@ def tile_mix_resid_fm_relu2_kernel(tc, x, w4_words, w4_scales, r8_words, r8_scal
             for m in (m0, m0 + 1):
                 add_w4(banks[m][:, HALF:T], m, 1, HALF)
                 add_r8(banks[m][:], m, 1, 0, stop=True)
+            for m in (m0, m0 + 1) if m0 == HALVED else (m0 + 1, m0):
                 relu_square(pair[:, m - m0, :], banks[m][:])
             nc.sync.dma_start(out=out[m0 * P : (m0 + 2) * P, :].rearrange("(m p) c -> p m c", p=P), in_=pair[:])
 

from contextlib import ExitStack

import concourse.mybir as mybir

K, N_OUT, T = 1024, 1536, 512
FLOPS = 2 * (2 * K * N_OUT * T)

F32 = mybir.dt.float32
BF16 = mybir.dt.bfloat16
I32 = mybir.dt.int32
U32 = mybir.dt.uint32
U8 = mybir.dt.uint8
E4M3 = mybir.dt.float8_e4m3fn_x4
E2M1 = mybir.dt.float4_e2m1fn_x4
ACT = mybir.ActivationFunctionType
ALU = mybir.AluOpType

P = 128
PACK = 4
K_PASS = P * PACK
PASSES = K // K_PASS
HALF = T // 2
N_TILES = N_OUT // P
BANKS = 8
ALIGN = 256
QUADRANTS = 4
W4_RUNS = ((0, BANKS * P), (BANKS * P, N_OUT))
R8_PLANES = 4
R8_PLANE_COLS = N_OUT // R8_PLANES
VECTOR_COLS = {P: 64, HALF: 144}
FIRST_VECTOR_COLS = 168
HALVED = 2
LAST_GROUPS = ((0, 256), (256, 128), (384, 128))
RESULTS = N_TILES + 4
WARM_WIDTHS = (256, 512, 512, 512, 512)
TWO_ONES = 0x3F803F80


def tile_mix_resid_fm_relu2_kernel(tc, x, w4_words, w4_scales, r8_words, r8_scales, out):
    nc = tc.nc

    with ExitStack() as ctx:
        keep = ctx.enter_context(tc.tile_pool(name="keep", bufs=1))
        work = ctx.enter_context(tc.tile_pool(name="work", bufs=RESULTS))
        psum = ctx.enter_context(tc.psum_pool(name="psum", bufs=1))
        ctx.enter_context(tc.manual_schedule())

        def open_bank(b):
            bank = psum.tile([P, T], F32, name="bank%d" % b)
            return bank

        w4_planes = [
            keep.tile([P, PASSES, n1 - n0], U8, name="w4_planes%d" % n0, align_bytes=ALIGN) for n0, n1 in W4_RUNS
        ]
        r8_planes = [keep.tile([P, R8_PLANE_COLS], U8, name="r8_planes%d" % a, align_bytes=ALIGN) for a in range(PASSES)]
        ones = keep.tile([P, PACK * HALF], BF16, name="ones", align_bytes=ALIGN)
        ones_codes = keep.tile([P, T], U32, name="ones_codes", align_bytes=ALIGN)
        ones_scales = keep.tile([P, T], U8, name="ones_scales", align_bytes=ALIGN)
        nc.vector.memset(w4_planes[0][:].bitcast(I32), 0)

        nc.vector.memset(ones[:].bitcast(I32), TWO_ONES)
        for c in (0, HALF):
            cols = slice(c, c + HALF)
            nc.vector.quantize_mx(out=ones_codes[:, cols].bitcast(E4M3), scales=ones_scales[:, cols], in_=ones[:])
        for plane in r8_planes + w4_planes[1:]:
            nc.vector.memset(plane[:].bitcast(I32), 0)
        unread = open_bank(BANKS - 1)
        for width in WARM_WIDTHS:
            nc.tensor.matmul_mx(
                out=unread[:, 0:width],
                lhsT=ones_codes[:, 0:P].bitcast(E4M3),
                lhsT_scale=ones_scales[:, 0:P],
                rhs=ones_codes[:, 0:width].bitcast(E4M3),
                rhs_scale=ones_scales[:, 0:width],
                start=True,
                stop=True,
            )

        def load_w4_scales(run):
            n0, n1 = W4_RUNS[run]
            for r in range(4):
                nc.sync.dma_start(
                    out=w4_planes[run][r:P:32, :, :].bitcast(I32),
                    in_=w4_scales.rearrange("a (q r) n -> r q a n", r=4)[r][:, :, n0:n1].bitcast(I32),
                )

        def load_r8_scales(a):
            for q in range(QUADRANTS):
                nc.sync.dma_start(
                    out=r8_planes[a][32 * q : 32 * q + 4 * R8_PLANES, :].bitcast(I32),
                    in_=r8_scales[a][4 * q : 4 * q + 4, :].rearrange("r (c n) -> c r n", c=R8_PLANES).bitcast(I32),
                )

        x_codes = [keep.tile([P, T], U32, name="x_codes%d" % a, align_bytes=ALIGN) for a in range(PASSES)]
        x_scales = [keep.tile([P, T], U8, name="x_scales%d" % a, align_bytes=ALIGN) for a in range(PASSES)]
        x_raw = {}

        def load_x(a, c, width):
            raw = keep.tile([P, PACK, width], F32, name="x_raw%d_%d" % (a, c), align_bytes=ALIGN)
            nc.sync.dma_start(
                out=raw[:],
                in_=x[a * K_PASS : (a + 1) * K_PASS, c : c + width].rearrange("(p j) w -> p j w", j=PACK),
            )
            x_raw[(a, c)] = raw

        def quantize_x(a, c):
            raw = x_raw[(a, c)]
            width = raw.shape[2]
            grouped = keep.tile([P, width, PACK], BF16, name="x_grouped%d_%d" % (a, c), align_bytes=ALIGN)

            def interleave(copy, c0, c1):
                copy(
                    out=grouped[:, c0:c1, :].rearrange("p (c i) j -> p c j i", i=4),
                    in_=raw[:, :, c0:c1].rearrange("p j (c i) -> p c j i", i=4),
                )

            if (a, c) == (0, 0):
                step = P
                interleave(nc.vector.tensor_copy, 0, P)
                interleave(nc.vector.tensor_copy, P, FIRST_VECTOR_COLS)
                interleave(nc.scalar.copy, FIRST_VECTOR_COLS, width)
            else:
                step = width
                interleave(nc.vector.tensor_copy, 0, VECTOR_COLS[width])
                interleave(nc.scalar.copy, VECTOR_COLS[width], width)
            for d in range(0, width, step):
                nc.vector.quantize_mx(
                    out=x_codes[a][:, c + d : c + d + step].bitcast(E4M3),
                    scales=x_scales[a][:, c + d : c + d + step],
                    in_=grouped[:, d : d + step, :].rearrange("p w j -> p (w j)"),
                )

        r8_parts = {}
        w4_parts = {}

        def load_r8(passes, m0, m1):
            words = keep.tile([P, len(passes), (m1 - m0) * P], U32, name="r8_%d_%d" % (passes[0], m0), align_bytes=ALIGN)
            rows = r8_words.rearrange("a p n i -> p a (n i)")[:, passes[0] : passes[-1] + 1, PACK * P * m0 : PACK * P * m1]
            nc.sync.dma_start(out=words[:].bitcast(I32), in_=rows.bitcast(I32))
            for i, a in enumerate(passes):
                for m in range(m0, m1):
                    r8_parts[(a, m)] = words[:, i, (m - m0) * P : (m - m0 + 1) * P].bitcast(E4M3)

        def load_w4(passes, m0, m1):
            words = keep.tile([P, len(passes), 2 * (m1 - m0) * P], U8, name="w4_%d_%d" % (passes[0], m0), align_bytes=ALIGN)
            rows = w4_words.rearrange("a p n -> p a n")[:, passes[0] : passes[-1] + 1, 2 * P * m0 : 2 * P * m1]
            nc.sync.dma_start(out=words[:].bitcast(I32), in_=rows.bitcast(I32))
            for i, a in enumerate(passes):
                for m in range(m0, m1):
                    w4_parts[(a, m)] = words[:, i, 2 * (m - m0) * P : 2 * (m - m0 + 1) * P].bitcast(E2M1)

        load_x(0, 0, HALF)
        load_w4_scales(0)
        load_w4((0,), 0, BANKS)
        load_x(0, HALF, P)
        load_x(0, T - P, P)
        load_r8((0,), 0, BANKS)
        load_r8_scales(0)
        load_x(1, 0, HALF)
        load_w4((1,), 0, BANKS)
        load_x(1, HALF, HALF)
        load_r8((1,), 0, BANKS // 2)
        load_r8_scales(1)
        load_r8((1,), BANKS // 2, BANKS)
        load_r8((0, 1), BANKS, N_TILES)
        load_w4((0, 1), BANKS, N_TILES)
        load_w4_scales(1)

        for a, c in x_raw:
            quantize_x(a, c)

        def add_r8(acc, m, a, c, start=False, stop=False):
            width = acc.shape[1]
            plane, col = divmod(m * P, R8_PLANE_COLS)
            nc.tensor.matmul_mx(
                out=acc,
                lhsT=r8_parts[(a, m)],
                lhsT_scale=r8_planes[a][4 * plane :, col : col + P],
                rhs=x_codes[a][:, c : c + width].bitcast(E4M3),
                rhs_scale=x_scales[a][:, c : c + width],
                start=start,
                stop=stop,
            )

        def add_w4(acc, m, a, c, start=False, stop=False):
            width = acc.shape[1]
            run, place = divmod(m, BANKS)
            nc.tensor.matmul_mx(
                out=acc,
                lhsT=w4_parts[(a, m)],
                lhsT_scale=w4_planes[run][:, a, place * P : (place + 1) * P],
                rhs=x_codes[a][:, c : c + width].bitcast(E4M3),
                rhs_scale=x_scales[a][:, c : c + width],
                start=start,
                stop=stop,
            )

        def buffer_like(acc):
            sums = work.tile([P, T], F32, name="sums", align_bytes=ALIGN)
            return sums[:, 0 : acc.shape[1]]

        def relu_square(result, acc):
            sums = buffer_like(acc)
            nc.scalar.copy(out=sums, in_=acc)
            nc.vector.scalar_tensor_tensor(out=result, in0=sums, scalar=0.0, in1=sums, op0=ALU.max, op1=ALU.mult)

        def finish(acc, m, c):
            width = acc.shape[1]
            result = keep.tile([P, width], F32, name="result%d_%d" % (m, c), align_bytes=ALIGN)
            relu_square(result[:], acc)
            nc.sync.dma_start(out=out[m * P : (m + 1) * P, c : c + width], in_=result[:])

        banks = [open_bank(m) for m in range(BANKS)]

        def place(m, c, width):
            if m < HALVED:
                col = m * HALF + c % HALF
                return banks[c // HALF][:, col : col + width]
            return banks[m][:, c : c + width]

        def finish_halves(h, steps=1):
            result = keep.tile([P, T], F32, name="halves%d" % h, align_bytes=ALIGN)
            for d in range(0, T, T // steps):
                cols = slice(d, d + T // steps)
                relu_square(result[:, cols], banks[h][:, cols])
            nc.sync.dma_start(
                out=out[0 : HALVED * P, h * HALF : (h + 1) * HALF].rearrange("(m p) c -> p m c", p=P),
                in_=result[:].rearrange("p (m c) -> p m c", m=HALVED),
            )

        for c in (0, P):
            for m in range(HALVED):
                add_w4(place(m, c, P), m, 0, c, start=(c == 0 and m == 0))
        for m in range(HALVED, BANKS):
            add_w4(place(m, 0, HALF), m, 0, 0, start=True)
        for c in (HALF, T - P):
            for m in range(BANKS):
                add_w4(place(m, c, P), m, 0, c, start=(c == HALF and m == 0))
        for m in range(HALVED):
            for c in (0, HALF):
                add_r8(place(m, c, HALF), m, 0, c)
        for m in range(HALVED, BANKS):
            add_r8(banks[m][:], m, 0, 0)

        for m in range(BANKS):
            add_w4(place(m, 0, HALF), m, 1, 0)
        for m in range(HALVED):
            add_r8(place(m, 0, HALF), m, 1, 0, stop=(m == HALVED - 1))
        finish_halves(0, steps=2)
        for m in range(HALVED):
            add_w4(place(m, HALF, HALF), m, 1, HALF)
            add_r8(place(m, HALF, HALF), m, 1, HALF, stop=(m == HALVED - 1))
        finish_halves(1)
        for m0 in range(HALVED, BANKS, 2):
            pair = keep.tile([P, 2, T], F32, name="pair%d" % m0, align_bytes=ALIGN)
            for m in (m0, m0 + 1):
                add_w4(banks[m][:, HALF:T], m, 1, HALF)
                add_r8(banks[m][:], m, 1, 0, stop=True)
            for m in (m0, m0 + 1) if m0 == HALVED else (m0 + 1, m0):
                relu_square(pair[:, m - m0, :], banks[m][:])
            nc.sync.dma_start(out=out[m0 * P : (m0 + 2) * P, :].rearrange("(m p) c -> p m c", p=P), in_=pair[:])

        for m in range(BANKS, N_TILES - 1):
            bank = open_bank(m - BANKS)
            for a in range(PASSES):
                add_r8(bank[:], m, a, 0, start=(a == 0))
                add_w4(bank[:], m, a, 0, stop=(a == PASSES - 1))
            if m < N_TILES - 2:
                finish(bank[:], m, 0)
            else:
                finish(bank[:, 0:HALF], m, 0)
                finish(bank[:, HALF:T], m, HALF)

        m = N_TILES - 1
        last = keep.tile([P, T], F32, name="last", align_bytes=ALIGN)
        for g, (c, width) in enumerate(LAST_GROUPS):
            bank = open_bank(m - BANKS + g)
            for a in range(PASSES):
                add_r8(bank[:, 0:width], m, a, c, start=(a == 0))
                add_w4(bank[:, 0:width], m, a, c, stop=(a == PASSES - 1))
            if c + width < T:
                relu_square(last[:, c : c + width], bank[:, 0:width])
            else:
                positive = buffer_like(bank[:, 0:width])
                nc.scalar.activation(out=positive, in_=bank[:, 0:width], func=ACT.Relu)
                nc.scalar.activation(out=last[:, c:T], in_=positive, func=ACT.Square)
            if (c + width) % HALF == 0:
                cols = slice(c + width - HALF, c + width)
                nc.sync.dma_start(out=out[m * P : (m + 1) * P, cols], in_=last[:, cols])
